import numpy as np, ml_dtypes
CORES = [113,118,241,246]
N = 4
BF = ml_dtypes.bfloat16
def f(rng, *shape):
    return (rng.standard_normal(shape, dtype=np.float32) * np.exp2(rng.integers(-2, 3, shape[:-1] + (1,)))).astype(BF)
def wide(rng, *shape):
    v = f(rng, *shape).astype(np.float32); k = shape[:-2] + (1, shape[-1])
    return (v * np.exp2(rng.integers(-6, 7, k)) * (rng.random(k) > 0.0625)).astype(BF)
M, K, TR, CAP = 2048, 48, 3, 288
D = 16 * K
def hashes(s, n):
    lo = ((s & 4095) + 1597 * n) & 4095; b = ((s >> 12) + ((lo * lo) >> 6)) & 4095
    return (lo + ((b * b) >> 6)) & 4095, b
def seed_of(a, b, n):
    lo = (a - ((b * b) >> 6)) & 4095
    return ((b - ((lo * lo) >> 6)) & 4095) * 4096 + ((lo - 1597 * n) & 4095)
def owners(t, s):
    a, b = hashes(np.asarray(s, np.int64)[..., None], (TR + 1) * np.arange(K)); w = (a * N) >> 12
    return np.where(b < t[w], w, t[N + w]).astype(np.int64)
def loads(t, s):
    o = owners(t, s); return np.stack([np.sum(o == q, -1) for q in range(N)], -1)
def sixteen(rng, t, keep=()):
    m = 16 - len(keep); kept = np.array(keep, np.int64); base = np.sum(loads(t, kept), 0)
    pool = rng.integers(0, 1 << 24, 1024); c = loads(t, pool); ok = np.flatnonzero(np.all(c * m <= CAP - base, 1)); j = np.arange(m)
    for u in range(m):
        if np.all(np.sum(c[j], 0) + base <= CAP): break
        j[u] = rng.choice(ok)
    return rng.permutation(np.concatenate([pool[j], kept]))
def ranks(rng, least):
    return np.concatenate([rng.integers(least, 4097, N), rng.permutation(N)]).astype(np.int64)
def absent(rng):
    w = rng.permutation(N); t = np.zeros(2 * N, np.int64)
    t[w] = (8192 * np.arange(N) + N - 1) // (2 * (N - 1)); t[N + w] = np.roll(w, -1); return t
def history(rng, dens):
    w = np.zeros((N, 128, M), np.float32)
    for q in range(N):
        for r in range(N):
            w[q] += np.float32(2 ** r) * (rng.random((128, M), dtype=np.float32) < dens[r][:, None])
    return w.astype(BF)
def seeds(rng, rk):
    return np.stack([np.stack([sixteen(rng, rk[g]) for g in range(8)]) for r in range(N)])
def complete(rng, rk, sd, dens=None):
    if dens is None: dens = rng.choice(np.array([0.1, 0.5, 0.9]), (N, 128))
    return {"sd": np.reshape(sd, (N, 128, 1)).astype(np.int32), "rk": np.stack([rk] * N).astype(np.int32), "thr": rng.integers(0, 4097, (N, 8, M)).astype(np.int32),
            "ali": rng.integers(0, M, (N, 8, M)).astype(np.int32), "seen": history(rng, dens), "vec": f(rng, N, 128, M)}
def setup_inputs(rng):
    rk = np.stack([ranks(rng, 2800) for g in range(8)]); return complete(rng, rk, seeds(rng, rk))
def setup_inputs_full(rng):
    o0 = rng.integers(0, N); rk = []
    for g in range(8):
        o = (o0 + g) % N; t = np.concatenate([rng.integers(3577 - 40, 3577 + 41, N), np.full(N, o)]).astype(np.int64); t[o] = 4096; rk.append(t)
    rk = np.stack(rk); sd = seeds(rng, rk); C = CAP // 16
    far = rng.integers(0, N, 8); h = rng.permutation(8); far[h[0]] = 0; far[h[1]] = rng.integers(1, N)
    for g in range(8):
        o = (o0 + g) % N; r = (o + far[g]) % N
        pool = rng.integers(0, 1 << 24, 4096); c = loads(rk[g], pool); fine = np.all(np.delete(c, o, 1) <= C, 1); s = []
        for i in range(8):
            x = rng.integers(-2, 3)
            for v in (C + x, C - x): s.append(pool[rng.choice(np.flatnonzero(fine & (c[:, o] == v)))])
        sd[r, g] = rng.permutation(np.array(s))
    return complete(rng, rk, sd)
def setup_inputs_edges(rng):
    rk, tie = [], []
    for g in range(8):
        t = ranks(rng, 3500); w = rng.permutation(N)[:4]; t[w[0]] = 0; t[N + w[0]] = w[1]; t[w[1]] = 0; t[N + w[1]] = w[0]; t[w[2]] = rng.integers(3500, 4096); t[N + w[2]] = w[0]; t[w[3]] = 4096; rk.append(t)
        tie.append(seed_of(int(w[2]) * (4096 // N) + int(rng.integers(0, 4096 // N)), int(t[w[2]]), (TR + 1) * int(rng.integers(0, K))))
    rk = np.stack(rk); sd = np.stack([np.stack([sixteen(rng, rk[g], (0, (1 << 24) - 1, tie[g])) for g in range(8)]) for r in range(N)])
    d = complete(rng, rk, sd); z = rng.integers(0, 4, (N, 8, M)); thr = np.where(z == 0, 0, np.where(z == 1, 4096, d["thr"])); z = rng.integers(0, 4, (N, 8, M))
    ali = np.where(z == 0, 0, np.where(z == 1, M - 1, np.where(z == 2, np.arange(M), d["ali"])))
    for r in range(N):
        for g in range(8):
            q = owners(rk[g], sd[r, g])[:, ::4]; a, b = hashes(sd[r, g][:, None], ((TR + 1) * np.arange(K) + 1)[None, ::4]); e = (a * M) >> 12
            thr[q, g, e] = b; ali[q, g, e] = M - 1 - e
    d["thr"] = thr.astype(np.int32); d["ali"] = ali.astype(np.int32); return d
def setup_inputs_hot(rng):
    rk = np.stack([ranks(rng, 2800) for g in range(8)]); sd = seeds(rng, rk)
    for g in range(8):
        pool = rng.integers(0, 1 << 24, 1024); sd[rng.integers(0, N), g] = pool[rng.choice(np.flatnonzero(np.all(loads(rk[g], pool) <= CAP // 16, 1)))]
    d = complete(rng, rk, sd); h = rng.integers(0, M, (N, 8, 1)); h[:, 0] = 0; h[:, 7] = M - 1
    d["thr"] = rng.integers(0, 512, (N, 8, M)).astype(np.int32); d["ali"] = (h + np.zeros((1, 1, M), np.int64)).astype(np.int32); return d
def setup_inputs_avid(rng):
    rk = np.stack([absent(rng) for g in range(8)]); dens = rng.choice(np.array([0, 0.97, 1.0]), (N, 128)); dens[rng.integers(0, N)] = 1
    return complete(rng, rk, seeds(rng, rk), dens)
def setup_inputs_spread(rng):
    d = setup_inputs(rng); d["vec"] = wide(rng, N, 128, M); d["thr"] = (4096 >> rng.integers(0, 14, (N, 8, M))).astype(np.int32); return d
def check_inputs(d):
    bad = []
    try:
        sd, rk = d["sd"].astype(np.int64), d["rk"].astype(np.int64); w = d["seen"].astype(np.float32)
        if not ((sd >= 0) & (sd < 1 << 24)).all(): bad.append("seed")
        if not (rk == rk[:1]).all(): bad.append("rk alike on all ranks")
        if not ((rk[..., :N] >= 0) & (rk[..., :N] <= 4096) & (rk[..., N:] >= 0) & (rk[..., N:] < N)).all(): bad.append("rk")
        if not ((d["thr"] >= 0) & (d["thr"] <= 4096)).all(): bad.append("thr")
        if not ((d["ali"] >= 0) & (d["ali"] < M)).all(): bad.append("ali")
        if not ((w >= 0) & (w < 2 ** N) & (w == np.floor(w))).all(): bad.append("seen")
        if not np.isfinite(d["vec"].astype(np.float32)).all(): bad.append("finite")
        if not bad and any((np.sum(loads(rk[r, g], sd[r, 16 * g:16 * g + 16, 0]), 0) > CAP).any() for r in range(N) for g in range(8)): bad.append("cap")
    except Exception:
        bad.append("unreadable")
    return bad
def reference(sd, rk, thr, ali, seen, vec):
    chosen = np.zeros((N, 128, K), np.float32); y = np.zeros((N, 128, D), vec.dtype); n = (TR + 1) * np.arange(K); row = np.arange(16)[:, None]
    for r in range(N):
        for g in range(8):
            s = sd[r, 16 * g:16 * g + 16].astype(np.int64)
            q = owners(rk[r, g].astype(np.int64), s[:, 0])
            x = np.zeros((16, K), np.int64); done = np.zeros((16, K), bool)
            for i in range(1, TR + 1):
                a, b = hashes(s, n + i); e = (a * M) >> 12
                c = np.where(b < thr[q, g, e], e, ali[q, g, e]).astype(np.int64)
                known = (seen[q, 16 * g + row, c].astype(np.float32).astype(np.int64) >> r) & 1
                x = np.where(done, x, c); done = done | (known == 0)
            chosen[r, 16 * g:16 * g + 16] = q * M + x
            y[r, 16 * g:16 * g + 16] = vec[q.T.reshape(-1), 16 * g + row, x.T.reshape(-1)]
    return {"chosen": chosen, "y": y}

@@ -1,0 +1,317 @@
+from concourse.bass import DstId, RemoteDMATransfer
+from concourse.mybir import AluOpType as OP, ActivationFunctionType as AF
+
+M, K, N = 2048, 48, 4
+J = 16 * K
+
+SCRATCH = {
+    "PW": ("sbuf", [128, 1024], "int32"), "SW": ("sbuf", [128, 4096], "bfloat16"), "VW": ("sbuf", [128, 8192], "bfloat16"),
+    "SEEN": ("sbuf", [128, 2048], "bfloat16"), "SDI": ("sbuf", [128, 1], "int32"), "RKI": ("sbuf", [8, 8], "int32"), "RKF": ("sbuf", [8, 8], "float32"),
+    "PI": ("sbuf", [128, 1], "int32"), "MI": ("sbuf", [128, 143], "int32"), "N0": ("sbuf", [128, 192], "int32"),
+    "PB": ("sbuf", [128, 8], "int32"), "PC": ("sbuf", [128, 16], "float32"), "M4": ("sbuf", [128, 128], "int32"),
+    "K0": ("sbuf", [128, 143], "float16"), "BO": ("sbuf", [128, 128], "bfloat16"), "ID": ("sbuf", [128, 128], "bfloat16"),
+    "ID16": ("sbuf", [128, 128], "bfloat16"), "IDH": ("sbuf", [128, 128], "float16"), "E8L": ("sbuf", [8, 128], "float32"),
+    "MOD": ("sbuf", [128, 16], "float32"), "DG": ("sbuf", [128, 2048], "bfloat16"),
+    "SI": ("sbuf", [128, 2], "int32"), "SF": ("sbuf", [128, 2], "float32"),
+    "L0": ("sbuf", [128, 192], "int32"), "L": ("sbuf", [128, 192], "int32"), "LL": ("sbuf", [128, 192], "int32"),
+    "TT": ("sbuf", [128, 192], "int32"), "B": ("sbuf", [128, 192], "int32"), "L64": ("sbuf", [128, 192], "int32"),
+    "BB": ("sbuf", [128, 192], "int32"), "AA": ("sbuf", [128, 192], "int32"),
+    "H": ("sbuf", [128, 144], "int32"), "HB": ("sbuf", [128, 144], "bfloat16"), "RM": ("sbuf", [128, 2304], "bfloat16"),
+    "W12": ("sbuf", [128, 48], "int32"), "VV": ("sbuf", [128, 48], "int32"), "TM": ("sbuf", [128, 336], "bfloat16"),
+    "CW": ("sbuf", [128, 4], "float32"), "CB": ("sbuf", [128, 4], "float32"), "A8": ("sbuf", [128, 4], "float32"),
+    "BP": ("sbuf", [128, 4], "float32"), "D1": ("sbuf", [128, 4], "float32"), "D2": ("sbuf", [128, 4], "float32"),
+    "LOW8": ("sbuf", [128, 144], "int32"), "EE": ("sbuf", [128, 144], "int32"), "EF": ("sbuf", [128, 144], "int32"),
+    "E8": ("sbuf", [128, 144], "int32"), "BQ": ("sbuf", [128, 144], "int32"), "S": ("sbuf", [128, 144], "int32"),
+    "E16": ("sbuf", [128, 144], "uint16"), "QH": ("sbuf", [128, 48], "float16"),
+    "MK": ("sbuf", [128, 2304], "bfloat16"), "X1": ("sbuf", [128, 2304], "float16"), "X2": ("sbuf", [128, 1536], "bfloat16"),
+    "CM": ("sbuf", [128, 144], "int32"), "DI": ("sbuf", [128, 144], "int32"), "AL": ("sbuf", [128, 144], "int32"),
+    "MM": ("sbuf", [128, 144], "int32"), "CC": ("sbuf", [128, 144], "int32"), "S1": ("sbuf", [128, 96], "int32"),
+    "S16": ("sbuf", [128, 96], "uint16"), "PAR": ("sbuf", [128, 96], "int32"), "PP": ("sbuf", [128, 96], "int32"),
+    "G": ("sbuf", [128, 144], "int32"), "GP": ("sbuf", [128, 144], "int32"), "TK": ("sbuf", [128, 96], "int32"),
+    "KB": ("sbuf", [128, 96], "int32"), "VAL": ("sbuf", [128, 96], "int32"), "MX": ("sbuf", [128, 96], "int32"),
+    "XG": ("sbuf", [128, 48], "int32"), "X16": ("sbuf", [128, 48], "uint16"), "CH": ("sbuf", [128, 48], "float32"),
+    "Y": ("sbuf", [128, 768], "bfloat16"),
+    "HR": ("psum", [128, 3072], "float32"), "RQ": ("psum", [128, 512], "float32"),
+}
+SEMAPHORES = ["v", "a", "t", "p", "lsd", "ltab", "lrk", "lseen", "lvec", "pk", "sn", "vp", "x0", "x1", "fw", "ls", "lf", "st"]
+
+
+def rank_program(g, core, T, topo):
+    r = T.rank_of(core)
+    if r is None:
+        return
+    others = [c for c in T.cores if c != core]
+    partner = [c for c in others if c in topo.cores_of(core)][0]
+    cross = [c for c in others if c != partner and topo.die(c) == topo.die(core)][0]
+    diag = [c for c in others if c not in (partner, cross)][0]
+    off = topo.engines(core, cross)
+    on = [e for e in topo.engines(core, partner) if e not in off]
+    bits = lambda es: sum(1 << e for e in es)
+    half = len(off) // 2
+    lanes = {partner: bits(on), cross: bits(off[:half]), diag: bits(off[half:])}
+    vec, act, pe = g.vector, g.scalar, g.tensor
+    cnt = {"v": 0, "a": 0, "t": 0, "p": 0}
+    lvl = {"v": {}, "a": {}, "t": {}, "p": {}, "s": {}}
+    eng = {"v": vec, "a": act, "t": pe, "p": g, "s": g.sync}
+
+    def need(q, deps):
+        for s, n in deps:
+            if lvl[q].get(s, 0) < n:
+                eng[q].wait_ge(T.sem[s], n)
+                lvl[q][s] = n
+
+    def run(q, call, deps, *args, **kw):
+        need(q, deps)
+        call(*args, **kw).then_inc(T.sem[q], 1)
+        cnt[q] += 1
+        return (q, cnt[q])
+
+    def V(call, deps, *args, **kw):
+        return run("v", call, deps, *args, **kw)
+
+    ts, tt, cp = vec.tensor_scalar, vec.tensor_tensor, vec.tensor_copy
+    SHR, AND = OP.arith_shift_right, OP.bitwise_and
+
+    my = slice(256 * r, 256 * r + 256)
+    g.sync.dma_start(T.SDI[:], T.sd[:]).then_inc(T.sem.lsd, 16)
+    act.dma_start(T.PW[1:128:2, my], T.ali[:]).then_inc(T.sem.ltab, 16)
+    g.sync.dma_start(T.PW[0:128:2, my], T.thr[:]).then_inc(T.sem.ltab, 16)
+    act.dma_start(T.RKI[:], T.rk[:]).then_inc(T.sem.lrk, 16)
+    g.sync.dma_start(T.SEEN[:], T.seen[:]).then_inc(T.sem.lseen, 16)
+    act.dma_start(T.VW[:, M * r:M * r + M], T.vec[:]).then_inc(T.sem.lvec, 16)
+
+    p1 = run("p", g.iota, [], T.PI[:], [[0, 1]], 0, 1)
+    p2 = run("p", g.iota, [], T.MI[:], [[1, 143]], 0, 0)
+    p3 = run("p", g.iota, [], T.N0[:], [[1597, 4], [6388, 48]], 0, 0)
+    PB, PC = T.PB, T.PC
+    V(ts, [p1], PB[:, 0:1], T.PI[:], 1, None, AND)
+    V(ts, [], PB[:, 1:2], T.PI[:], 112, None, AND)
+    V(ts, [], PB[:, 2:3], T.PI[:], 15, None, AND)
+    a = V(ts, [], PB[:, 3:4], T.PI[:], 1, 7, SHR, AND)
+    bias = V(ts, [a], PC[:, 0:1], PB[:, 0:1], 2048.0, -2048.0, OP.mult, OP.add)
+    V(ts, [], PC[:, 1:2], PB[:, 0:1], -8191.0, 8192.0, OP.mult, OP.add)
+    V(ts, [], PC[:, 2:3], PB[:, 1:2], 15.0, None, OP.add)
+    V(cp, [], PC[:, 3:4], PB[:, 1:2])
+    V(cp, [], PC[:, 4:5], PB[:, 2:3])
+    V(cp, [], PC[:, 5:6], PB[:, 3:4])
+    V(cp, [], PC[:, 6:7], T.PI[:])
+    a = V(ts, [], PC[:, 7:8], T.PI[:], 16.0, None, OP.mult)
+    V(ts, [p2], T.M4[:], T.MI[:, 0:128], 112, None, AND)
+    idt = V(ts, [a], T.ID[:], T.MI[:, 0:128], PC[:, 6:7], None, OP.is_equal)
+    mod = V(ts, [], T.MOD[:], T.MI[:, 0:16], PC[:, 4:5], None, OP.is_equal)
+    id16 = V(ts, [], T.ID16[:], T.MI[:, 0:128], PC[:, 6:7], 16.0, OP.is_equal, OP.mult)
+    e8l = V(ts, [("v", cnt["v"])], T.E8L[:], T.M4[0:8, :], PC[0:8, 7:8], None, OP.is_equal)
+    V(ts, [], T.BO[:], T.M4[:], PC[:, 3:4], None, OP.is_equal)
+    V(ts, [], T.K0[:], T.MI[:], PC[:, 2:3], PC[:, 1:2], OP.is_equal, OP.mult)
+    V(ts, [], T.IDH[:], T.MI[:, 0:128], PC[:, 6:7], None, OP.is_equal)
+    V(ts, [], T.CW[:], T.MI[:, 0:4], 2048.0, None, OP.mult)
+    cst = V(ts, [], T.CB[:], T.MI[:, 0:4], 4096.0, None, OP.mult)
+
+    V(ts, [("lsd", 16)], T.SI[:, 0:1], T.SDI[:], 4095, None, AND)
+    a = V(ts, [], T.SI[:, 1:2], T.SDI[:], 12, None, SHR)
+    V(cp, [a], T.SF[:, 0:1], T.SI[:, 0:1])
+    sf = V(ts, [], T.SF[:, 1:2], T.SI[:, 1:2], 64.0, -262144.0, OP.mult, OP.add)
+    a = V(ts, [p3, sf], T.L0[:], T.N0[:], T.SF[:, 0:1], None, OP.add)
+    tab = V(ts, [("ltab", 32)], T.PW[:, my], T.PW[:, my], PC[:, 0:1], None, OP.add)
+    a = V(ts, [a], T.L[:], T.L0[:], 4095, None, AND)
+    rkf = V(cp, [("lrk", 16)], T.RKF[:], T.RKI[:])
+    ll = V(tt, [a], T.LL[:], T.L[:], T.L[:], OP.mult)
+    V(ts, [], T.L64[:], T.L[:], 64.0, -262144.0, OP.mult, OP.add)
+    a = V(ts, [ll], T.TT[:], T.LL[:], T.SF[:, 1:2], None, OP.add)
+    b = V(ts, [a], T.B[:], T.TT[:], 6, 4095, SHR, AND)
+    a = V(tt, [b], T.BB[:], T.B[:], T.B[:], OP.mult)
+    need("t", [e8l, rkf])
+    pe.matmul(T.RQ[:, 0:8], T.E8L[:], T.RKF[:], True, True).then_inc(T.sem.t, 1)
+    cnt["t"] += 1
+    rt = ("t", cnt["t"])
+    V(ts, [rt], T.A8[:], T.RQ[:, 4:8], 2048.0, None, OP.mult)
+    a8 = V(tt, [], T.BP[:], T.RQ[:, 0:4], T.CB[:], OP.add)
+    aa = V(tt, [a], T.AA[:], T.BB[:], T.L64[:], OP.add)
+    V(tt, [a8], T.D1[:], T.A8[:], T.CW[:], OP.subtract)
+    dd = V(tt, [], T.D2[:, 0:3], T.CW[:, 1:4], T.A8[:, 0:3], OP.subtract)
+    a = V(ts, [aa], T.H[:], T.AA[:, 48:192], 15, 7, SHR, AND)
+    w12 = V(ts, [], T.W12[:], T.AA[:, 0:48], 4, 3 << 12, SHR, AND)
+    hb = V(cp, [a], T.HB[:], T.H[:])
+    vv = V(tt, [w12], T.VV[:], T.W12[:], T.B[:, 0:48], OP.add)
+
+    def diagonals(us):
+        t = None
+        for u in us:
+            t = run("a", act.activation, [idt, mod], T.DG[:, 128 * u:128 * u + 128], T.ID[:], AF.Copy, scale=T.MOD[:, u:u + 1])
+        return t
+
+    diagonals(range(0, 8))
+    mine = range(10, 16)
+    ea = None
+    for u in mine:
+        ea = run("a", act.activation, [hb], T.RM[:, u:3 * J:16], T.HB[:], AF.Copy, scale=T.MOD[:, u:u + 1])
+    ev = None
+    for u in range(16):
+        if u not in mine:
+            ev = V(ts, [hb], T.RM[:, u:3 * J:16], T.HB[:], T.MOD[:, u:u + 1], None, OP.mult)
+    need("t", [("lseen", 16), id16])
+    packs = []
+    for hf in range(2):
+        o = T.HR[:, 2048 + 512 * hf:2560 + 512 * hf]
+        pe.matmul(o, T.ID[:], T.SEEN[:, 1024 * hf:1024 * hf + 1024:2], True, False)
+        pe.matmul(o, T.ID16[:], T.SEEN[:, 1024 * hf + 1:1024 * hf + 1024:2], False, True).then_inc(T.sem.t, 1)
+        cnt["t"] += 1
+        packs.append(("t", cnt["t"]))
+    pk2 = None
+    for hf in range(2):
+        pk2 = run("a", act.activation, [packs[hf]], T.SW[:, 1024 * r + 512 * hf:1024 * r + 512 * hf + 512], T.HR[:, 2048 + 512 * hf:2560 + 512 * hf], AF.Copy)
+    dgt = diagonals(range(8, 16))
+
+    def spread(buf, a0, a1, sem):
+        tr = []
+        for d in (cross, diag, partner):
+            rid, pid = topo.addr(d, core)
+            tr.append(RemoteDMATransfer(dst_ids=[DstId(rid=rid, pnc=pid)], dma_engine_mask=lanes[d], remote_sem=T.sem[sem],
+                                        srcs=[T[buf][:, a0:a1]], dsts=[T[buf][:, a0:a1]]))
+        g.remote_dma_fused(tr, local_sem=T.sem.ls)
+
+    need("p", [tab])
+    spread("PW", 256 * r, 256 * r + 256, "pk")
+    need("p", [pk2])
+    spread("SW", 1024 * r, 1024 * r + 1024, "sn")
+    need("p", [("lvec", 16)])
+    for c in range(2):
+        a0 = M * r + 1024 * c
+        tr = []
+        for d, es, sem in ((cross, off, "x%d" % c), (partner, on, "vp")):
+            rid, pid = topo.addr(d, core)
+            tr.append(RemoteDMATransfer(dst_ids=[DstId(rid=rid, pnc=pid)], dma_engine_mask=bits(es), remote_sem=T.sem[sem],
+                                        srcs=[T.VW[:, a0:a0 + 1024]], dsts=[T.VW[:, a0:a0 + 1024]]))
+        g.remote_dma_fused(tr, local_sem=T.sem.ls)
+    rid, pid = topo.addr(partner, core)
+    for c in range(2):
+        need("p", [("x%d" % c, len(off))])
+        a0 = M * T.rank_of(cross) + 1024 * c
+        g.remote_dma(T.VW[:, a0:a0 + 1024], T.VW[:, a0:a0 + 1024], T.sem.fw, T.sem.lf, pid, rid, bits(on))
+
+    def spread_h(i, deps):
+        need("t", deps)
+        pe.matmul(T.HR[:, 1024 * i:1024 * i + 512], T.BO[:], T.RM[:, J * i:J * i + 512], True, True)
+        pe.matmul(T.HR[:, 1024 * i + 512:1024 * i + 768], T.BO[:], T.RM[:, J * i + 512:J * i + 768], True, True).then_inc(T.sem.t, 1)
+        cnt["t"] += 1
+        return ("t", cnt["t"])
+
+    hr = [spread_h(0, [ea, ev, cst])]
+    steps = []
+    for w in range(4):
+        steps.append(V(ts, [vv, dd], T.TM[:, 48 * w:48 * w + 48], T.VV[:], T.BP[:, w:w + 1], T.D1[:, w:w + 1], OP.is_ge, OP.mult))
+    for w in range(3):
+        steps.append(V(ts, [], T.TM[:, 192 + 48 * w:240 + 48 * w], T.VV[:], 4096.0 * (w + 1), T.D2[:, w:w + 1], OP.is_ge, OP.mult))
+    Q8 = T.RQ[:, 64:112]
+    for w in range(7):
+        need("t", [steps[w]])
+        m = pe.matmul(Q8, T.ID[:], T.TM[:, 48 * w:48 * w + 48], w == 0, w == 6)
+    m.then_inc(T.sem.t, 1)
+    cnt["t"] += 1
+    qt = ("t", cnt["t"])
+    hr.append(spread_h(1, []))
+    hr.append(spread_h(2, [pk2]))
+    low = V(ts, [], T.LOW8[:], T.AA[:, 48:192], 4, 255 << 3, SHR, AND)
+    ee = V(ts, [], T.EE[:], T.AA[:, 48:192], 7, 2047, SHR, AND)
+    V(ts, [], T.BQ[:], T.B[:, 48:192], 8192.0, -2047.0 * 8192.0, OP.mult, OP.add)
+
+    def blk(i):
+        return slice(48 * i, 48 * i + 48)
+
+    def mask(i):
+        return V(ts, [hr[i]], T.MK[:, J * i:J * i + J], T.HR[:, 1024 * i:1024 * i + 768], PC[:, 5:6], None, OP.is_equal)
+
+    mk = [mask(0)]
+    ef = V(ts, [ee], T.EF[:], T.EE[:], 8192.0, None, OP.add)
+    s = [V(tt, [qt, low], T.S[:, blk(i)], T.LOW8[:, blk(i)], Q8, OP.add) for i in range(3)]
+    qh = V(cp, [], T.QH[:], Q8)
+    e16 = V(ts, [s[2]], T.E16[:], T.S[:], 0.125, None, OP.mult)
+    e8 = [V(tt, [ef], T.E8[:, blk(i)], T.EF[:, blk(i)], Q8, OP.add) for i in range(3)]
+    mk.append(mask(1))
+
+    def look(i):
+        x = V(tt, [("pk", 16), mk[i], e16], T.X1[:, J * i:J * i + J], T.PW[:].indirect(T.E16[:, blk(i)]), T.MK[:, J * i:J * i + J], OP.mult)
+        need("t", [x])
+        o = T.HR[:, 1024 * i + 768:1024 * i + 816]
+        pe.matmul(o, T.IDH[:], T.QH[:], True, False)
+        for u in range(16):
+            m = pe.matmul(o, T.K0[:, 15 - u:143 - u], T.X1[:, J * i + u:J * i + J:16], False, u == 15)
+        m.then_inc(T.sem.t, 1)
+        cnt["t"] += 1
+        return ("t", cnt["t"])
+
+    def resolve(i, d):
+        o = T.HR[:, 1024 * i + 768:1024 * i + 816]
+        di = V(cp, [d], T.DI[:, blk(i)], o)
+        cm = V(tt, [], T.CM[:, blk(i)], o, T.BQ[:, blk(i)], OP.is_ge)
+        al = V(ts, [di], T.AL[:, blk(i)], T.DI[:, blk(i)], 8191, None, AND)
+        mm = V(tt, [cm, e8[i]], T.MM[:, blk(i)], T.CM[:, blk(i)], T.E8[:, blk(i)], OP.mult)
+        cc = V(tt, [mm], T.CC[:, blk(i)], T.AL[:, blk(i)], T.MM[:, blk(i)], OP.max)
+        s16 = None
+        if i < 2:
+            s1 = V(ts, [cc], T.S1[:, blk(i)], T.CC[:, blk(i)], 8191, 1, AND, SHR)
+            s16 = V(cp, [s1], T.S16[:, blk(i)], T.S1[:, blk(i)])
+        return cc, s16
+
+    PRI = (1 << 15, 1 << 14, 1 << 13)
+
+    def prepare(i, cc):
+        gi = V(ts, [cc], T.G[:, blk(i)], T.CC[:, blk(i)], 8191, None, AND)
+        if i < 2:
+            V(ts, [], T.PAR[:, blk(i)], T.CC[:, blk(i)], 1, None, AND)
+        t = V(ts, [gi], T.GP[:, blk(i)], T.G[:, blk(i)], float(PRI[i]), None, OP.add)
+        if i < 2:
+            t = V(ts, [t], T.PP[:, blk(i)], T.PAR[:, blk(i)], float(-15 * (PRI[i] >> (r + 4))), float(PRI[i] >> r), OP.mult, OP.add)
+        return t
+
+    def history(i, deps):
+        need("t", deps)
+        o = T.HR[:, 1024 * i:1024 * i + 48]
+        for u in range(16):
+            m = pe.matmul(o, T.DG[:, 128 * u:128 * u + 128], T.X2[:, J * i + u:J * i + J:16], u == 0, u == 15)
+        m.then_inc(T.sem.t, 1)
+        cnt["t"] += 1
+        return ("t", cnt["t"])
+
+    def known(i, d, pp):
+        o = T.HR[:, 1024 * i:1024 * i + 48]
+        t = V(tt, [d, pp], T.TK[:, blk(i)], o, T.PP[:, blk(i)], OP.mult)
+        t = V(ts, [t], T.KB[:, blk(i)], T.TK[:, blk(i)], PRI[i], None, AND)
+        return V(tt, [t], T.VAL[:, blk(i)], T.GP[:, blk(i)], T.KB[:, blk(i)], OP.subtract)
+
+    d0 = look(0)
+    d1 = look(1)
+    mk.append(mask(2))
+    cc0, s0 = resolve(0, d0)
+    x0 = run("a", act.activation, [("sn", 16), s0, dgt], T.X2[:, 0:J], T.SW[:].indirect(T.S16[:, 0:48]), AF.Copy)
+    pp0 = prepare(0, cc0)
+    cc1, s1 = resolve(1, d1)
+    x1a = run("a", act.activation, [s1], T.X2[:, J + 384:2 * J], T.SW[:].indirect(T.S16[:, 72:96]), AF.Copy)
+    x1v = V(cp, [("sn", 16), s1], T.X2[:, J:J + 384], T.SW[:].indirect(T.S16[:, 48:72]))
+    k0 = history(0, [x0, dgt])
+    d2 = look(2)
+    k1 = history(1, [x1a, x1v])
+    pp1 = prepare(1, cc1)
+    v0 = known(0, k0, pp0)
+    cc2, _ = resolve(2, d2)
+    g2 = prepare(2, cc2)
+    m0 = V(tt, [g2, v0], T.MX[:, 0:48], T.VAL[:, 0:48], T.GP[:, 96:144], OP.max)
+    v1 = known(1, k1, pp1)
+    t = V(tt, [v1, m0], T.MX[:, 48:96], T.MX[:, 0:48], T.VAL[:, 48:96], OP.max)
+    t = V(ts, [t], T.XG[:], T.MX[:, 48:96], 8191, None, AND)
+    t = V(cp, [t], T.X16[:], T.XG[:])
+
+    here = [("lvec", 16), ("vp", 2 * len(on)), ("x0", len(off)), ("x1", len(off)), ("fw", 2 * len(on))]
+    ya = run("a", act.activation, here + [t], T.Y[:, 384:768], T.VW[:].indirect(T.X16[:, 24:48]), AF.Copy)
+    yv = V(cp, here + [t], T.Y[:, 0:384], T.VW[:].indirect(T.X16[:, 0:24]))
+    ch = V(cp, [t], T.CH[:], T.XG[:])
+    need("a", [ya])
+    act.dma_start(T.y[:, 384:768], T.Y[:, 384:768]).then_inc(T.sem.st, 16)
+    need("s", [yv])
+    g.sync.dma_start(T.y[:, 0:384], T.Y[:, 0:384]).then_inc(T.sem.st, 16)
+    need("s", [ch])
+    g.sync.dma_start(T.chosen[:], T.CH[:]).then_inc(T.sem.st, 16)
+
+    need("p", [(q, cnt[q]) for q in ("v", "a", "t", "p")])
+    need("p", [("ls", 4 * 16), ("lf", 2 * len(on)), ("vp", 2 * len(on)), ("fw", 2 * len(on)), ("pk", 16), ("sn", 16), ("st", 48)])
+    need("p", [("lsd", 16), ("ltab", 32), ("lrk", 16), ("lseen", 16), ("lvec", 16)])

@@ -3,37 +3,28 @@ from concourse.mybir import AluOpType as OP, ActivationFunctionType as AF
 
 M, K, N = 2048, 48, 4
 J = 16 * K
+CUTS = (0, 896, 1536, 2048)
 
-SCRATCH = {
-    "PW": ("sbuf", [128, 1024], "int32"), "SW": ("sbuf", [128, 4096], "bfloat16"), "VW": ("sbuf", [128, 8192], "bfloat16"),
-    "SEEN": ("sbuf", [128, 2048], "bfloat16"), "SDI": ("sbuf", [128, 1], "int32"), "RKI": ("sbuf", [8, 8], "int32"), "RKF": ("sbuf", [8, 8], "float32"),
-    "PI": ("sbuf", [128, 1], "int32"), "MI": ("sbuf", [128, 143], "int32"), "N0": ("sbuf", [128, 192], "int32"),
-    "PB": ("sbuf", [128, 8], "int32"), "PC": ("sbuf", [128, 16], "float32"), "M4": ("sbuf", [128, 128], "int32"),
-    "K0": ("sbuf", [128, 143], "float16"), "BO": ("sbuf", [128, 128], "bfloat16"), "ID": ("sbuf", [128, 128], "bfloat16"),
-    "ID16": ("sbuf", [128, 128], "bfloat16"), "IDH": ("sbuf", [128, 128], "float16"), "E8L": ("sbuf", [8, 128], "float32"),
-    "MOD": ("sbuf", [128, 16], "float32"), "DG": ("sbuf", [128, 2048], "bfloat16"),
-    "SI": ("sbuf", [128, 2], "int32"), "SF": ("sbuf", [128, 2], "float32"),
-    "L0": ("sbuf", [128, 192], "int32"), "L": ("sbuf", [128, 192], "int32"), "LL": ("sbuf", [128, 192], "int32"),
-    "TT": ("sbuf", [128, 192], "int32"), "B": ("sbuf", [128, 192], "int32"), "L64": ("sbuf", [128, 192], "int32"),
-    "BB": ("sbuf", [128, 192], "int32"), "AA": ("sbuf", [128, 192], "int32"),
-    "H": ("sbuf", [128, 144], "int32"), "HB": ("sbuf", [128, 144], "bfloat16"), "RM": ("sbuf", [128, 2304], "bfloat16"),
-    "W12": ("sbuf", [128, 48], "int32"), "VV": ("sbuf", [128, 48], "int32"), "TM": ("sbuf", [128, 336], "bfloat16"),
-    "CW": ("sbuf", [128, 4], "float32"), "CB": ("sbuf", [128, 4], "float32"), "A8": ("sbuf", [128, 4], "float32"),
-    "BP": ("sbuf", [128, 4], "float32"), "D1": ("sbuf", [128, 4], "float32"), "D2": ("sbuf", [128, 4], "float32"),
-    "LOW8": ("sbuf", [128, 144], "int32"), "EE": ("sbuf", [128, 144], "int32"), "EF": ("sbuf", [128, 144], "int32"),
-    "E8": ("sbuf", [128, 144], "int32"), "BQ": ("sbuf", [128, 144], "int32"), "S": ("sbuf", [128, 144], "int32"),
-    "E16": ("sbuf", [128, 144], "uint16"), "QH": ("sbuf", [128, 48], "float16"),
-    "MK": ("sbuf", [128, 2304], "bfloat16"), "X1": ("sbuf", [128, 2304], "float16"), "X2": ("sbuf", [128, 1536], "bfloat16"),
-    "CM": ("sbuf", [128, 144], "int32"), "DI": ("sbuf", [128, 144], "int32"), "AL": ("sbuf", [128, 144], "int32"),
-    "MM": ("sbuf", [128, 144], "int32"), "CC": ("sbuf", [128, 144], "int32"), "S1": ("sbuf", [128, 96], "int32"),
-    "S16": ("sbuf", [128, 96], "uint16"), "PAR": ("sbuf", [128, 96], "int32"), "PP": ("sbuf", [128, 96], "int32"),
-    "G": ("sbuf", [128, 144], "int32"), "GP": ("sbuf", [128, 144], "int32"), "TK": ("sbuf", [128, 96], "int32"),
-    "KB": ("sbuf", [128, 96], "int32"), "VAL": ("sbuf", [128, 96], "int32"), "MX": ("sbuf", [128, 96], "int32"),
-    "XG": ("sbuf", [128, 48], "int32"), "X16": ("sbuf", [128, 48], "uint16"), "CH": ("sbuf", [128, 48], "float32"),
-    "Y": ("sbuf", [128, 768], "bfloat16"),
-    "HR": ("psum", [128, 3072], "float32"), "RQ": ("psum", [128, 512], "float32"),
-}
-SEMAPHORES = ["v", "a", "t", "p", "lsd", "ltab", "lrk", "lseen", "lvec", "pk", "sn", "vp", "x0", "x1", "fw", "ls", "lf", "st"]
+I4, F4, F2, H2 = "int32", "float32", "bfloat16", "float16"
+SCRATCH = {n: ("sbuf", [p, c], d) for n, p, c, d in (
+    ("PW", 128, 1024, I4), ("SW", 128, 4096, F2), ("VW", 128, 8192, F2), ("SEEN", 128, 2048, F2), ("SDI", 128, 1, I4),
+    ("RKI", 8, 8, I4), ("RKF", 8, 8, F4), ("PI", 128, 1, I4), ("MI", 128, 143, I4), ("N0", 128, 192, I4), ("PB", 128, 8, I4),
+    ("PC", 128, 16, F4), ("M4", 128, 128, I4), ("K0", 128, 143, H2), ("BO", 128, 128, F2), ("ID", 128, 128, F2),
+    ("ID16", 128, 128, F2), ("IDH", 128, 128, H2), ("E8L", 8, 128, F4), ("MOD", 128, 16, F4), ("DG", 128, 2048, F2),
+    ("SI", 128, 2, I4), ("SF", 128, 2, F4), ("L0", 128, 192, I4), ("L", 128, 192, I4), ("LL", 128, 192, I4), ("TT", 128, 192, I4),
+    ("B", 128, 192, I4), ("BB", 128, 192, I4), ("AA", 128, 192, I4), ("H", 128, 144, I4), ("HB", 128, 144, F2),
+    ("RM", 128, 2304, F2), ("W12", 128, 48, I4), ("VV", 128, 48, I4), ("TM", 128, 336, F2), ("CW", 128, 4, F4), ("CB", 128, 4, F4),
+    ("A8", 128, 4, F4), ("BP", 128, 4, F4), ("D1", 128, 4, F4), ("D2", 128, 4, F4), ("LOW8", 128, 144, I4), ("EE", 128, 144, I4),
+    ("EF", 128, 144, I4), ("E8", 128, 144, I4), ("BQ", 128, 144, I4), ("S", 128, 144, I4), ("E16", 128, 144, "uint16"),
+    ("QH", 128, 48, H2), ("AB", 128, 1536, F2), ("MK", 128, 2304, F2), ("X1", 128, 2304, H2), ("X2", 128, 1536, F2),
+    ("CM", 128, 144, I4), ("DI", 128, 144, I4), ("AL", 128, 144, I4), ("MM", 128, 144, I4), ("CC", 128, 144, I4), ("S1", 128, 96, I4),
+    ("S16", 128, 96, "uint16"), ("PAR", 128, 96, I4), ("PP", 128, 96, I4), ("GP", 128, 144, I4), ("TK", 128, 96, I4),
+    ("KB", 128, 96, I4), ("VAL", 128, 96, I4), ("MX", 128, 96, I4), ("XG", 128, 48, I4), ("X16", 128, 48, "uint16"),
+    ("CH", 128, 48, F4), ("Y", 128, 768, F2))}
+SCRATCH["HR"] = ("psum", [128, 3072], F4)
+SCRATCH["RQ"] = ("psum", [128, 512], F4)
+SCRATCH["DA"] = ("psum", [128, 512], F4)
+SEMAPHORES = ["v", "a", "t", "p", "lsd", "ltab", "lrk", "lseen", "lvec", "pk", "sn", "vp", "x0", "x1", "x2", "fw", "ls", "lf", "st"]
 
 
 def rank_program(g, core, T, topo):
@@ -45,7 +36,8 @@ def rank_program(g, core, T, topo):
     cross = [c for c in others if c != partner and topo.die(c) == topo.die(core)][0]
     diag = [c for c in others if c not in (partner, cross)][0]
     off = topo.engines(core, cross)
-    on = [e for e in topo.engines(core, partner) if e not in off]
+    near = topo.engines(core, partner)
+    on = [e for e in near if e not in off]
     bits = lambda es: sum(1 << e for e in es)
     half = len(off) // 2
     lanes = {partner: bits(on), cross: bits(off[:half]), diag: bits(off[half:])}
@@ -66,8 +58,22 @@ def rank_program(g, core, T, topo):
         cnt[q] += 1
         return (q, cnt[q])
 
-    def V(call, deps, *args, **kw):
-        return run("v", call, deps, *args, **kw)
+    def V(call, deps, *args):
+        return run("v", call, deps, *args)
+
+    def A(deps, *args, **kw):
+        return run("a", act.activation, deps, *args, **kw)
+
+    def closed(m):
+        m.then_inc(T.sem.t, 1)
+        cnt["t"] += 1
+        return ("t", cnt["t"])
+
+    def blk(i):
+        return slice(48 * i, 48 * i + 48)
+
+    def pos(i):
+        return slice(J * i, J * i + J)
 
     ts, tt, cp = vec.tensor_scalar, vec.tensor_tensor, vec.tensor_copy
     SHR, AND = OP.arith_shift_right, OP.bitwise_and
@@ -78,29 +84,30 @@ def rank_program(g, core, T, topo):
     g.sync.dma_start(T.PW[0:128:2, my], T.thr[:]).then_inc(T.sem.ltab, 16)
     act.dma_start(T.RKI[:], T.rk[:]).then_inc(T.sem.lrk, 16)
     g.sync.dma_start(T.SEEN[:], T.seen[:]).then_inc(T.sem.lseen, 16)
-    act.dma_start(T.VW[:, M * r:M * r + M], T.vec[:]).then_inc(T.sem.lvec, 16)
+    g.sync.dma_start(T.VW[:, M * r:M * r + M], T.vec[:]).then_inc(T.sem.lvec, 16)
 
     p1 = run("p", g.iota, [], T.PI[:], [[0, 1]], 0, 1)
     p2 = run("p", g.iota, [], T.MI[:], [[1, 143]], 0, 0)
     p3 = run("p", g.iota, [], T.N0[:], [[1597, 4], [6388, 48]], 0, 0)
     PB, PC = T.PB, T.PC
-    V(ts, [p1], PB[:, 0:1], T.PI[:], 1, None, AND)
+    V(ts, [p1], PB[:, 2:3], T.PI[:], 15, None, AND)
     V(ts, [], PB[:, 1:2], T.PI[:], 112, None, AND)
-    V(ts, [], PB[:, 2:3], T.PI[:], 15, None, AND)
-    a = V(ts, [], PB[:, 3:4], T.PI[:], 1, 7, SHR, AND)
-    bias = V(ts, [a], PC[:, 0:1], PB[:, 0:1], 2048.0, -2048.0, OP.mult, OP.add)
+    V(ts, [], PB[:, 0:1], T.PI[:], 1, None, AND)
+    V(ts, [], PB[:, 3:4], T.PI[:], 1, 7, SHR, AND)
+    V(cp, [], PC[:, 6:7], T.PI[:])
+    V(cp, [("v", 2)], PC[:, 3:4], PB[:, 1:2])
+    a = V(cp, [], PC[:, 4:5], PB[:, 2:3])
+    V(ts, [a, p2], T.ID[:], T.MI[:, 0:128], PC[:, 6:7], None, OP.is_equal)
+    idt = V(ts, [], T.MOD[:], T.MI[:, 0:16], PC[:, 4:5], None, OP.is_equal)
+    V(ts, [], PC[:, 0:1], PB[:, 0:1], 2048.0, -2048.0, OP.mult, OP.add)
     V(ts, [], PC[:, 1:2], PB[:, 0:1], -8191.0, 8192.0, OP.mult, OP.add)
     V(ts, [], PC[:, 2:3], PB[:, 1:2], 15.0, None, OP.add)
-    V(cp, [], PC[:, 3:4], PB[:, 1:2])
-    V(cp, [], PC[:, 4:5], PB[:, 2:3])
     V(cp, [], PC[:, 5:6], PB[:, 3:4])
-    V(cp, [], PC[:, 6:7], T.PI[:])
-    a = V(ts, [], PC[:, 7:8], T.PI[:], 16.0, None, OP.mult)
-    V(ts, [p2], T.M4[:], T.MI[:, 0:128], 112, None, AND)
-    idt = V(ts, [a], T.ID[:], T.MI[:, 0:128], PC[:, 6:7], None, OP.is_equal)
-    mod = V(ts, [], T.MOD[:], T.MI[:, 0:16], PC[:, 4:5], None, OP.is_equal)
+    V(ts, [], PC[:, 8:9], PB[:, 3:4], -1.0, None, OP.mult)
+    V(ts, [], PC[:, 7:8], T.PI[:], 16.0, None, OP.mult)
+    a = V(ts, [], T.M4[:], T.MI[:, 0:128], 112, None, AND)
     id16 = V(ts, [], T.ID16[:], T.MI[:, 0:128], PC[:, 6:7], 16.0, OP.is_equal, OP.mult)
-    e8l = V(ts, [("v", cnt["v"])], T.E8L[:], T.M4[0:8, :], PC[0:8, 7:8], None, OP.is_equal)
+    e8l = V(ts, [a], T.E8L[:], T.M4[0:8, :], PC[0:8, 7:8], None, OP.is_equal)
     V(ts, [], T.BO[:], T.M4[:], PC[:, 3:4], None, OP.is_equal)
     V(ts, [], T.K0[:], T.MI[:], PC[:, 2:3], PC[:, 1:2], OP.is_equal, OP.mult)
     V(ts, [], T.IDH[:], T.MI[:, 0:128], PC[:, 6:7], None, OP.is_equal)
@@ -109,209 +116,156 @@ def rank_program(g, core, T, topo):
 
     V(ts, [("lsd", 16)], T.SI[:, 0:1], T.SDI[:], 4095, None, AND)
     a = V(ts, [], T.SI[:, 1:2], T.SDI[:], 12, None, SHR)
-    V(cp, [a], T.SF[:, 0:1], T.SI[:, 0:1])
-    sf = V(ts, [], T.SF[:, 1:2], T.SI[:, 1:2], 64.0, -262144.0, OP.mult, OP.add)
-    a = V(ts, [p3, sf], T.L0[:], T.N0[:], T.SF[:, 0:1], None, OP.add)
+    b = V(cp, [a], T.SF[:, 0:1], T.SI[:, 0:1])
+    V(ts, [], T.SF[:, 1:2], T.SI[:, 1:2], 64.0, -262144.0, OP.mult, OP.add)
+    a = V(ts, [p3, b], T.L0[:], T.N0[:], T.SF[:, 0:1], None, OP.add)
     tab = V(ts, [("ltab", 32)], T.PW[:, my], T.PW[:, my], PC[:, 0:1], None, OP.add)
     a = V(ts, [a], T.L[:], T.L0[:], 4095, None, AND)
     rkf = V(cp, [("lrk", 16)], T.RKF[:], T.RKI[:])
     ll = V(tt, [a], T.LL[:], T.L[:], T.L[:], OP.mult)
-    V(ts, [], T.L64[:], T.L[:], 64.0, -262144.0, OP.mult, OP.add)
+    L64 = T.DA[:, 128:320]
+    V(ts, [], L64, T.L[:], 64.0, -262144.0, OP.mult, OP.add)
     a = V(ts, [ll], T.TT[:], T.LL[:], T.SF[:, 1:2], None, OP.add)
-    b = V(ts, [a], T.B[:], T.TT[:], 6, 4095, SHR, AND)
-    a = V(tt, [b], T.BB[:], T.B[:], T.B[:], OP.mult)
     need("t", [e8l, rkf])
-    pe.matmul(T.RQ[:, 0:8], T.E8L[:], T.RKF[:], True, True).then_inc(T.sem.t, 1)
-    cnt["t"] += 1
-    rt = ("t", cnt["t"])
+    rt = closed(pe.matmul(T.RQ[:, 0:8], T.E8L[:], T.RKF[:], True, True))
+    b = V(ts, [a], T.B[:], T.TT[:], 6, 4095, SHR, AND)
     V(ts, [rt], T.A8[:], T.RQ[:, 4:8], 2048.0, None, OP.mult)
+    a = V(tt, [b], T.BB[:], T.B[:], T.B[:], OP.mult)
     a8 = V(tt, [], T.BP[:], T.RQ[:, 0:4], T.CB[:], OP.add)
-    aa = V(tt, [a], T.AA[:], T.BB[:], T.L64[:], OP.add)
+    aa = V(tt, [a], T.AA[:], T.BB[:], L64, OP.add)
     V(tt, [a8], T.D1[:], T.A8[:], T.CW[:], OP.subtract)
     dd = V(tt, [], T.D2[:, 0:3], T.CW[:, 1:4], T.A8[:, 0:3], OP.subtract)
-    a = V(ts, [aa], T.H[:], T.AA[:, 48:192], 15, 7, SHR, AND)
+    h = V(ts, [aa], T.H[:], T.AA[:, 48:192], 15, 7, SHR, AND)
     w12 = V(ts, [], T.W12[:], T.AA[:, 0:48], 4, 3 << 12, SHR, AND)
-    hb = V(cp, [a], T.HB[:], T.H[:])
+    hb = V(cp, [h], T.HB[:], T.H[:])
     vv = V(tt, [w12], T.VV[:], T.W12[:], T.B[:, 0:48], OP.add)
+    low = V(ts, [], T.LOW8[:], T.AA[:, 48:192], 4, 255 << 3, SHR, AND)
 
-    def diagonals(us):
-        t = None
-        for u in us:
-            t = run("a", act.activation, [idt, mod], T.DG[:, 128 * u:128 * u + 128], T.ID[:], AF.Copy, scale=T.MOD[:, u:u + 1])
-        return t
-
-    diagonals(range(0, 8))
-    mine = range(10, 16)
-    ea = None
-    for u in mine:
-        ea = run("a", act.activation, [hb], T.RM[:, u:3 * J:16], T.HB[:], AF.Copy, scale=T.MOD[:, u:u + 1])
-    ev = None
     for u in range(16):
-        if u not in mine:
-            ev = V(ts, [hb], T.RM[:, u:3 * J:16], T.HB[:], T.MOD[:, u:u + 1], None, OP.mult)
+        dg = A([idt], T.DG[:, 128 * u:128 * u + 128], T.ID[:], AF.Copy, scale=T.MOD[:, u:u + 1])
     need("t", [("lseen", 16), id16])
-    packs = []
     for hf in range(2):
         o = T.HR[:, 2048 + 512 * hf:2560 + 512 * hf]
         pe.matmul(o, T.ID[:], T.SEEN[:, 1024 * hf:1024 * hf + 1024:2], True, False)
-        pe.matmul(o, T.ID16[:], T.SEEN[:, 1024 * hf + 1:1024 * hf + 1024:2], False, True).then_inc(T.sem.t, 1)
-        cnt["t"] += 1
-        packs.append(("t", cnt["t"]))
-    pk2 = None
-    for hf in range(2):
-        pk2 = run("a", act.activation, [packs[hf]], T.SW[:, 1024 * r + 512 * hf:1024 * r + 512 * hf + 512], T.HR[:, 2048 + 512 * hf:2560 + 512 * hf], AF.Copy)
-    dgt = diagonals(range(8, 16))
+        c = closed(pe.matmul(o, T.ID16[:], T.SEEN[:, 1024 * hf + 1:1024 * hf + 1024:2], False, True))
+        packed = A([c], T.SW[:, 1024 * r + 512 * hf:1024 * r + 512 * hf + 512], o, AF.Copy)
 
-    def spread(buf, a0, a1, sem):
+    Q8 = T.RQ[:, 64:112]
+    for w in range(7):
+        o = T.TM[:, 48 * w:48 * w + 48]
+        if w < 4:
+            c = V(ts, [vv, dd], o, T.VV[:], T.BP[:, w:w + 1], T.D1[:, w:w + 1], OP.is_ge, OP.mult)
+        else:
+            c = V(ts, [], o, T.VV[:], 4096.0 * (w - 3), T.D2[:, w - 4:w - 3], OP.is_ge, OP.mult)
+        need("t", [c])
+        m = pe.matmul(Q8, T.ID[:], o, w == 0, w == 6)
+    qt = closed(m)
+    for u in range(16):
+        if u < 8:
+            ev = V(ts, [hb], T.RM[:, u:3 * J:16], T.HB[:], T.MOD[:, u:u + 1], None, OP.mult)
+        else:
+            ea = A([hb], T.RM[:, u:3 * J:16], T.HB[:], AF.Copy, scale=T.MOD[:, u:u + 1])
+
+    def send(buf, a0, a1, dests):
         tr = []
-        for d in (cross, diag, partner):
+        for d, mask, sem in dests:
             rid, pid = topo.addr(d, core)
-            tr.append(RemoteDMATransfer(dst_ids=[DstId(rid=rid, pnc=pid)], dma_engine_mask=lanes[d], remote_sem=T.sem[sem],
+            tr.append(RemoteDMATransfer(dst_ids=[DstId(rid=rid, pnc=pid)], dma_engine_mask=mask, remote_sem=T.sem[sem],
                                         srcs=[T[buf][:, a0:a1]], dsts=[T[buf][:, a0:a1]]))
         g.remote_dma_fused(tr, local_sem=T.sem.ls)
 
     need("p", [tab])
-    spread("PW", 256 * r, 256 * r + 256, "pk")
-    need("p", [pk2])
-    spread("SW", 1024 * r, 1024 * r + 1024, "sn")
+    send("PW", 256 * r, 256 * r + 256, [(d, lanes[d], "pk") for d in (cross, diag, partner)])
+    need("p", [packed])
+    send("SW", 1024 * r, 1024 * r + 1024, [(d, lanes[d], "sn") for d in (cross, diag, partner)])
     need("p", [("lvec", 16)])
-    for c in range(2):
-        a0 = M * r + 1024 * c
-        tr = []
-        for d, es, sem in ((cross, off, "x%d" % c), (partner, on, "vp")):
-            rid, pid = topo.addr(d, core)
-            tr.append(RemoteDMATransfer(dst_ids=[DstId(rid=rid, pnc=pid)], dma_engine_mask=bits(es), remote_sem=T.sem[sem],
-                                        srcs=[T.VW[:, a0:a0 + 1024]], dsts=[T.VW[:, a0:a0 + 1024]]))
-        g.remote_dma_fused(tr, local_sem=T.sem.ls)
+    pieces = list(zip(CUTS, CUTS[1:]))
+    n = len(pieces)
+    for c, (a0, a1) in enumerate(pieces):
+        send("VW", M * r + a0, M * r + a1, [(cross, bits(off), "x%d" % c), (partner, bits(on), "vp")])
     rid, pid = topo.addr(partner, core)
-    for c in range(2):
+    for c, (a0, a1) in enumerate(pieces):
         need("p", [("x%d" % c, len(off))])
-        a0 = M * T.rank_of(cross) + 1024 * c
-        g.remote_dma(T.VW[:, a0:a0 + 1024], T.VW[:, a0:a0 + 1024], T.sem.fw, T.sem.lf, pid, rid, bits(on))
+        w = slice(M * T.rank_of(cross) + a0, M * T.rank_of(cross) + a1)
+        g.remote_dma(T.VW[:, w], T.VW[:, w], T.sem.fw, T.sem.lf, pid, rid, bits(on if c < n - 1 else near))
+    handed = (n - 1) * len(on) + len(near)
 
-    def spread_h(i, deps):
-        need("t", deps)
+    hr = []
+    for i in range(3):
+        need("t", [ea, ev, cst] + ([packed] if i == 2 else []))
         pe.matmul(T.HR[:, 1024 * i:1024 * i + 512], T.BO[:], T.RM[:, J * i:J * i + 512], True, True)
-        pe.matmul(T.HR[:, 1024 * i + 512:1024 * i + 768], T.BO[:], T.RM[:, J * i + 512:J * i + 768], True, True).then_inc(T.sem.t, 1)
-        cnt["t"] += 1
-        return ("t", cnt["t"])
-
-    hr = [spread_h(0, [ea, ev, cst])]
-    steps = []
-    for w in range(4):
-        steps.append(V(ts, [vv, dd], T.TM[:, 48 * w:48 * w + 48], T.VV[:], T.BP[:, w:w + 1], T.D1[:, w:w + 1], OP.is_ge, OP.mult))
-    for w in range(3):
-        steps.append(V(ts, [], T.TM[:, 192 + 48 * w:240 + 48 * w], T.VV[:], 4096.0 * (w + 1), T.D2[:, w:w + 1], OP.is_ge, OP.mult))
-    Q8 = T.RQ[:, 64:112]
-    for w in range(7):
-        need("t", [steps[w]])
-        m = pe.matmul(Q8, T.ID[:], T.TM[:, 48 * w:48 * w + 48], w == 0, w == 6)
-    m.then_inc(T.sem.t, 1)
-    cnt["t"] += 1
-    qt = ("t", cnt["t"])
-    hr.append(spread_h(1, []))
-    hr.append(spread_h(2, [pk2]))
-    low = V(ts, [], T.LOW8[:], T.AA[:, 48:192], 4, 255 << 3, SHR, AND)
+        hr.append(closed(pe.matmul(T.HR[:, 1024 * i + 512:1024 * i + 768], T.BO[:], T.RM[:, J * i + 512:J * i + 768], True, True)))
+    for i in range(3):
+        s = V(tt, [qt, low], T.S[:, blk(i)], T.LOW8[:, blk(i)], Q8, OP.add)
+    V(cp, [], T.QH[:], Q8)
+    e16 = V(ts, [s], T.E16[:], T.S[:], 0.125, None, OP.mult)
     ee = V(ts, [], T.EE[:], T.AA[:, 48:192], 7, 2047, SHR, AND)
     V(ts, [], T.BQ[:], T.B[:, 48:192], 8192.0, -2047.0 * 8192.0, OP.mult, OP.add)
-
-    def blk(i):
-        return slice(48 * i, 48 * i + 48)
-
-    def mask(i):
-        return V(ts, [hr[i]], T.MK[:, J * i:J * i + J], T.HR[:, 1024 * i:1024 * i + 768], PC[:, 5:6], None, OP.is_equal)
-
-    mk = [mask(0)]
+    mk = [V(ts, [hr[0]], T.MK[:, pos(0)], T.HR[:, 0:768], PC[:, 5:6], None, OP.is_equal)]
+    for i in (1, 2):
+        c = A([hr[i]], T.AB[:, pos(i - 1)], T.HR[:, 1024 * i:1024 * i + 768], AF.Abs, bias=PC[:, 8:9])
+        mk.append(A([c], T.MK[:, pos(i)], T.AB[:, pos(i - 1)], AF.Relu, bias=1.0, scale=-1.0))
     ef = V(ts, [ee], T.EF[:], T.EE[:], 8192.0, None, OP.add)
-    s = [V(tt, [qt, low], T.S[:, blk(i)], T.LOW8[:, blk(i)], Q8, OP.add) for i in range(3)]
-    qh = V(cp, [], T.QH[:], Q8)
-    e16 = V(ts, [s[2]], T.E16[:], T.S[:], 0.125, None, OP.mult)
-    e8 = [V(tt, [ef], T.E8[:, blk(i)], T.EF[:, blk(i)], Q8, OP.add) for i in range(3)]
-    mk.append(mask(1))
+
+    D = [T.DA[:, 0:48], T.DA[:, 48:96], T.HR[:, 2816:2864]]
 
     def look(i):
-        x = V(tt, [("pk", 16), mk[i], e16], T.X1[:, J * i:J * i + J], T.PW[:].indirect(T.E16[:, blk(i)]), T.MK[:, J * i:J * i + J], OP.mult)
+        x = V(tt, [("pk", 16), mk[i], e16], T.X1[:, pos(i)], T.PW[:].indirect(T.E16[:, blk(i)]), T.MK[:, pos(i)], OP.mult)
         need("t", [x])
-        o = T.HR[:, 1024 * i + 768:1024 * i + 816]
-        pe.matmul(o, T.IDH[:], T.QH[:], True, False)
+        pe.matmul(D[i], T.IDH[:], T.QH[:], True, False)
         for u in range(16):
-            m = pe.matmul(o, T.K0[:, 15 - u:143 - u], T.X1[:, J * i + u:J * i + J:16], False, u == 15)
-        m.then_inc(T.sem.t, 1)
-        cnt["t"] += 1
-        return ("t", cnt["t"])
+            m = pe.matmul(D[i], T.K0[:, 15 - u:143 - u], T.X1[:, J * i + u:J * i + J:16], False, u == 15)
+        return closed(m)
 
-    def resolve(i, d):
-        o = T.HR[:, 1024 * i + 768:1024 * i + 816]
-        di = V(cp, [d], T.DI[:, blk(i)], o)
-        cm = V(tt, [], T.CM[:, blk(i)], o, T.BQ[:, blk(i)], OP.is_ge)
-        al = V(ts, [di], T.AL[:, blk(i)], T.DI[:, blk(i)], 8191, None, AND)
-        mm = V(tt, [cm, e8[i]], T.MM[:, blk(i)], T.CM[:, blk(i)], T.E8[:, blk(i)], OP.mult)
-        cc = V(tt, [mm], T.CC[:, blk(i)], T.AL[:, blk(i)], T.MM[:, blk(i)], OP.max)
-        s16 = None
-        if i < 2:
-            s1 = V(ts, [cc], T.S1[:, blk(i)], T.CC[:, blk(i)], 8191, 1, AND, SHR)
-            s16 = V(cp, [s1], T.S16[:, blk(i)], T.S1[:, blk(i)])
-        return cc, s16
+    def resolve(w, o, d):
+        di = V(cp, [d], T.DI[:, w], o)
+        cm = V(tt, [], T.CM[:, w], o, T.BQ[:, w], OP.is_ge)
+        V(ts, [di], T.AL[:, w], T.DI[:, w], 8191, None, AND)
+        mm = V(tt, [cm], T.MM[:, w], T.CM[:, w], T.E8[:, w], OP.mult)
+        return V(tt, [mm], T.CC[:, w], T.AL[:, w], T.MM[:, w], OP.max)
 
-    PRI = (1 << 15, 1 << 14, 1 << 13)
-
-    def prepare(i, cc):
-        gi = V(ts, [cc], T.G[:, blk(i)], T.CC[:, blk(i)], 8191, None, AND)
-        if i < 2:
-            V(ts, [], T.PAR[:, blk(i)], T.CC[:, blk(i)], 1, None, AND)
-        t = V(ts, [gi], T.GP[:, blk(i)], T.G[:, blk(i)], float(PRI[i]), None, OP.add)
-        if i < 2:
-            t = V(ts, [t], T.PP[:, blk(i)], T.PAR[:, blk(i)], float(-15 * (PRI[i] >> (r + 4))), float(PRI[i] >> r), OP.mult, OP.add)
-        return t
-
-    def history(i, deps):
-        need("t", deps)
-        o = T.HR[:, 1024 * i:1024 * i + 48]
-        for u in range(16):
-            m = pe.matmul(o, T.DG[:, 128 * u:128 * u + 128], T.X2[:, J * i + u:J * i + J:16], u == 0, u == 15)
-        m.then_inc(T.sem.t, 1)
-        cnt["t"] += 1
-        return ("t", cnt["t"])
-
-    def known(i, d, pp):
-        o = T.HR[:, 1024 * i:1024 * i + 48]
-        t = V(tt, [d, pp], T.TK[:, blk(i)], o, T.PP[:, blk(i)], OP.mult)
-        t = V(ts, [t], T.KB[:, blk(i)], T.TK[:, blk(i)], PRI[i], None, AND)
-        return V(tt, [t], T.VAL[:, blk(i)], T.GP[:, blk(i)], T.KB[:, blk(i)], OP.subtract)
-
-    d0 = look(0)
-    d1 = look(1)
-    mk.append(mask(2))
-    cc0, s0 = resolve(0, d0)
-    x0 = run("a", act.activation, [("sn", 16), s0, dgt], T.X2[:, 0:J], T.SW[:].indirect(T.S16[:, 0:48]), AF.Copy)
-    pp0 = prepare(0, cc0)
-    cc1, s1 = resolve(1, d1)
-    x1a = run("a", act.activation, [s1], T.X2[:, J + 384:2 * J], T.SW[:].indirect(T.S16[:, 72:96]), AF.Copy)
-    x1v = V(cp, [("sn", 16), s1], T.X2[:, J:J + 384], T.SW[:].indirect(T.S16[:, 48:72]))
-    k0 = history(0, [x0, dgt])
+    look(0)
+    for i in range(3):
+        e8 = V(tt, [ef], T.E8[:, blk(i)], T.EF[:, blk(i)], Q8, OP.add)
+    d01 = look(1)
     d2 = look(2)
-    k1 = history(1, [x1a, x1v])
-    pp1 = prepare(1, cc1)
-    v0 = known(0, k0, pp0)
-    cc2, _ = resolve(2, d2)
-    g2 = prepare(2, cc2)
-    m0 = V(tt, [g2, v0], T.MX[:, 0:48], T.VAL[:, 0:48], T.GP[:, 96:144], OP.max)
-    v1 = known(1, k1, pp1)
-    t = V(tt, [v1, m0], T.MX[:, 48:96], T.MX[:, 0:48], T.VAL[:, 48:96], OP.max)
-    t = V(ts, [t], T.XG[:], T.MX[:, 48:96], 8191, None, AND)
+    two = slice(0, 96)
+    need("v", [e8])
+    cc = resolve(two, T.DA[:, two], d01)
+    c = V(ts, [cc], T.S1[:], T.CC[:, two], 8191, 1, AND, SHR)
+    par = V(ts, [], T.PAR[:], T.CC[:, two], 1, None, AND)
+    s16 = V(cp, [c], T.S16[:], T.S1[:])
+    xa = A([s16, ("sn", 16)], T.X2[:, pos(0)], T.SW[:].indirect(T.S16[:, blk(0)]), AF.Copy)
+    xv = V(cp, [s16, ("sn", 16)], T.X2[:, pos(1)], T.SW[:].indirect(T.S16[:, blk(1)]))
+    need("t", [xa, xv, dg])
+    D2 = T.HR[:, two]
+    for u in range(16):
+        m = pe.matmul(D2, T.DG[:, 128 * u:128 * u + 128], T.X2[:, u:2 * J:16], u == 0, u == 15)
+    kn = closed(m)
+    V(ts, [], T.GP[:, blk(0)], T.CC[:, blk(0)], 65536.0 + 16384.0, None, OP.add)
+    V(ts, [], T.GP[:, blk(1)], T.CC[:, blk(1)], 65536.0, None, OP.add)
+    pp = V(ts, [par], T.PP[:], T.PAR[:], float(-15 * (65536 >> (r + 4))), float(65536 >> r), OP.mult, OP.add)
+    cc = resolve(blk(2), D[2], d2)
+    g2 = V(ts, [cc], T.GP[:, blk(2)], T.CC[:, blk(2)], 32768.0, None, OP.add)
+    t = V(tt, [kn, pp], T.TK[:], D2, T.PP[:], OP.mult)
+    t = V(ts, [t], T.KB[:], T.TK[:], 65536, None, AND)
+    t = V(tt, [t], T.VAL[:], T.GP[:, two], T.KB[:], OP.subtract)
+    t = V(tt, [t, g2], T.MX[:, blk(0)], T.VAL[:, blk(0)], T.VAL[:, blk(1)], OP.max)
+    t = V(tt, [t], T.MX[:, blk(1)], T.MX[:, blk(0)], T.GP[:, blk(2)], OP.max)
+    t = V(ts, [t], T.XG[:], T.MX[:, blk(1)], 8191, None, AND)
     t = V(cp, [t], T.X16[:], T.XG[:])
 
-    here = [("lvec", 16), ("vp", 2 * len(on)), ("x0", len(off)), ("x1", len(off)), ("fw", 2 * len(on))]
-    ya = run("a", act.activation, here + [t], T.Y[:, 384:768], T.VW[:].indirect(T.X16[:, 24:48]), AF.Copy)
+    here = [("lvec", 16), ("vp", n * len(on))] + [("x%d" % c, len(off)) for c in range(n)] + [("fw", handed)]
+    ya = A(here + [t], T.Y[:, 384:768], T.VW[:].indirect(T.X16[:, 24:48]), AF.Copy)
+    ch = V(cp, [], T.CH[:], T.XG[:])
     yv = V(cp, here + [t], T.Y[:, 0:384], T.VW[:].indirect(T.X16[:, 0:24]))
-    ch = V(cp, [t], T.CH[:], T.XG[:])
+    need("s", [ch])
+    g.sync.dma_start(T.chosen[:], T.CH[:]).then_inc(T.sem.st, 16)
     need("a", [ya])
     act.dma_start(T.y[:, 384:768], T.Y[:, 384:768]).then_inc(T.sem.st, 16)
     need("s", [yv])
     g.sync.dma_start(T.y[:, 0:384], T.Y[:, 0:384]).then_inc(T.sem.st, 16)
-    need("s", [ch])
-    g.sync.dma_start(T.chosen[:], T.CH[:]).then_inc(T.sem.st, 16)
 
     need("p", [(q, cnt[q]) for q in ("v", "a", "t", "p")])
-    need("p", [("ls", 4 * 16), ("lf", 2 * len(on)), ("vp", 2 * len(on)), ("fw", 2 * len(on)), ("pk", 16), ("sn", 16), ("st", 48)])
+    need("p", [("ls", (2 + n) * 16), ("lf", handed), ("vp", n * len(on)), ("fw", handed), ("pk", 16), ("sn", 16), ("st", 48)])
     need("p", [("lsd", 16), ("ltab", 32), ("lrk", 16), ("lseen", 16), ("lvec", 16)])

@@ -4,26 +4,29 @@ from concourse.mybir import AluOpType as OP, ActivationFunctionType as AF
 M, K, N = 2048, 48, 4
 J = 16 * K
 CUTS = (0, 896, 1536, 2048)
+YV = 22
+EARLY = 3
 
-I4, F4, F2, H2 = "int32", "float32", "bfloat16", "float16"
+I4, F4, F2, H2, U2 = "int32", "float32", "bfloat16", "float16", "uint16"
 SCRATCH = {n: ("sbuf", [p, c], d) for n, p, c, d in (
     ("PW", 128, 1024, I4), ("SW", 128, 4096, F2), ("VW", 128, 8192, F2), ("SEEN", 128, 2048, F2), ("SDI", 128, 1, I4),
-    ("RKI", 8, 8, I4), ("RKF", 8, 8, F4), ("PI", 128, 1, I4), ("MI", 128, 143, I4), ("N0", 128, 192, I4), ("PB", 128, 8, I4),
-    ("PC", 128, 16, F4), ("M4", 128, 128, I4), ("K0", 128, 143, H2), ("BO", 128, 128, F2), ("ID", 128, 128, F2),
-    ("ID16", 128, 128, F2), ("IDH", 128, 128, H2), ("E8L", 8, 128, F4), ("MOD", 128, 16, F4), ("DG", 128, 2048, F2),
-    ("SI", 128, 2, I4), ("SF", 128, 2, F4), ("L0", 128, 192, I4), ("L", 128, 192, I4), ("LL", 128, 192, I4), ("TT", 128, 192, I4),
-    ("B", 128, 192, I4), ("BB", 128, 192, I4), ("AA", 128, 192, I4), ("H", 128, 144, I4), ("HB", 128, 144, F2),
-    ("RM", 128, 2304, F2), ("W12", 128, 48, I4), ("VV", 128, 48, I4), ("TM", 128, 336, F2), ("CW", 128, 4, F4), ("CB", 128, 4, F4),
-    ("A8", 128, 4, F4), ("BP", 128, 4, F4), ("D1", 128, 4, F4), ("D2", 128, 4, F4), ("LOW8", 128, 144, I4), ("EE", 128, 144, I4),
-    ("EF", 128, 144, I4), ("E8", 128, 144, I4), ("BQ", 128, 144, I4), ("S", 128, 144, I4), ("E16", 128, 144, "uint16"),
-    ("QH", 128, 48, H2), ("AB", 128, 1536, F2), ("MK", 128, 2304, F2), ("X1", 128, 2304, H2), ("X2", 128, 1536, F2),
-    ("CM", 128, 144, I4), ("DI", 128, 144, I4), ("AL", 128, 144, I4), ("MM", 128, 144, I4), ("CC", 128, 144, I4), ("S1", 128, 96, I4),
-    ("S16", 128, 96, "uint16"), ("PAR", 128, 96, I4), ("PP", 128, 96, I4), ("GP", 128, 144, I4), ("TK", 128, 96, I4),
-    ("KB", 128, 96, I4), ("VAL", 128, 96, I4), ("MX", 128, 96, I4), ("XG", 128, 48, I4), ("X16", 128, 48, "uint16"),
-    ("CH", 128, 48, F4), ("Y", 128, 768, F2))}
-SCRATCH["HR"] = ("psum", [128, 3072], F4)
+    ("RKI", 8, 8, I4), ("RKF", 8, 8, F4), ("TI", 128, 24, I4), ("TA", 128, 24, I4), ("T8", 128, 8, I4), ("TS", 128, 8, I4),
+    ("MI", 128, 128, F4), ("AB", 128, 128, F2), ("N0", 128, 192, I4), ("EI", 8, 128, F4), ("EA", 8, 128, F4), ("PB", 128, 1, I4),
+    ("PC", 128, 1, F4), ("K0", 128, 144, H2), ("ID", 128, 128, F2), ("ID16", 128, 128, F2), ("IDN", 128, 128, H2),
+    ("E8L", 8, 128, F4), ("MOD", 128, 16, F4), ("MW", 128, 8, F2), ("DG", 128, 2048, F2), ("SI", 128, 1, I4), ("SF", 128, 2, F4),
+    ("L0", 128, 192, I4), ("L", 128, 192, I4), ("LL", 128, 192, F4), ("TT", 128, 192, I4), ("B", 128, 192, I4),
+    ("BB", 128, 192, I4), ("AA", 128, 192, I4), ("H", 128, 144, I4), ("H16", 128, 144, U2), ("W12", 128, 48, I4),
+    ("VV", 128, 48, I4), ("TM", 128, 336, F2), ("CW", 128, 4, F4), ("CB", 128, 4, F4), ("A8", 128, 4, F4), ("BP", 128, 4, F4),
+    ("D1", 128, 4, F4), ("D2", 128, 4, F4), ("LOW8", 128, 144, I4), ("EE", 128, 144, I4), ("BH", 128, 144, H2),
+    ("S", 128, 144, I4), ("E16", 128, 144, U2), ("MK", 128, 2304, F2), ("X1", 128, 2304, H2), ("X2", 128, 1536, F2),
+    ("M1", 128, 144, I4), ("C1", 128, 144, I4), ("C2", 128, 96, I4), ("S2", 128, 96, I4), ("S16", 128, 96, U2), ("PAR", 128, 96, I4),
+    ("PP", 128, 96, I4), ("TK", 128, 96, I4), ("KB", 128, 96, I4), ("VAL", 128, 96, F4), ("MX", 128, 48, I4), ("XG", 128, 48, I4),
+    ("X16", 128, 48, U2), ("CH", 128, 48, F4), ("Y", 128, 768, F2))}
+SCRATCH["HP"] = ("psum", [128, 1024], F4)
+SCRATCH["HU"] = ("psum", [128, 512], F4)
+SCRATCH["DD"] = ("psum", [128, 1024], F4)
 SCRATCH["RQ"] = ("psum", [128, 512], F4)
-SCRATCH["DA"] = ("psum", [128, 512], F4)
+SCRATCH["VB"] = ("psum", [128, 512], F4)
 SEMAPHORES = ["v", "a", "t", "p", "lsd", "ltab", "lrk", "lseen", "lvec", "pk", "sn", "vp", "x0", "x1", "x2", "fw", "ls", "lf", "st"]
 
 
@@ -77,6 +80,7 @@ def rank_program(g, core, T, topo):
 
     ts, tt, cp = vec.tensor_scalar, vec.tensor_tensor, vec.tensor_copy
     SHR, AND = OP.arith_shift_right, OP.bitwise_and
+    two = slice(0, 96)
 
     my = slice(256 * r, 256 * r + 256)
     g.sync.dma_start(T.SDI[:], T.sd[:]).then_inc(T.sem.lsd, 16)
@@ -86,69 +90,68 @@ def rank_program(g, core, T, topo):
     g.sync.dma_start(T.SEEN[:], T.seen[:]).then_inc(T.sem.lseen, 16)
     g.sync.dma_start(T.VW[:, M * r:M * r + M], T.vec[:]).then_inc(T.sem.lvec, 16)
 
-    p1 = run("p", g.iota, [], T.PI[:], [[0, 1]], 0, 1)
-    p2 = run("p", g.iota, [], T.MI[:], [[1, 143]], 0, 0)
-    p3 = run("p", g.iota, [], T.N0[:], [[1597, 4], [6388, 48]], 0, 0)
-    PB, PC = T.PB, T.PC
-    V(ts, [p1], PB[:, 2:3], T.PI[:], 15, None, AND)
-    V(ts, [], PB[:, 1:2], T.PI[:], 112, None, AND)
-    V(ts, [], PB[:, 0:1], T.PI[:], 1, None, AND)
-    V(ts, [], PB[:, 3:4], T.PI[:], 1, 7, SHR, AND)
-    V(cp, [], PC[:, 6:7], T.PI[:])
-    V(cp, [("v", 2)], PC[:, 3:4], PB[:, 1:2])
-    a = V(cp, [], PC[:, 4:5], PB[:, 2:3])
-    V(ts, [a, p2], T.ID[:], T.MI[:, 0:128], PC[:, 6:7], None, OP.is_equal)
-    idt = V(ts, [], T.MOD[:], T.MI[:, 0:16], PC[:, 4:5], None, OP.is_equal)
-    V(ts, [], PC[:, 0:1], PB[:, 0:1], 2048.0, -2048.0, OP.mult, OP.add)
-    V(ts, [], PC[:, 1:2], PB[:, 0:1], -8191.0, 8192.0, OP.mult, OP.add)
-    V(ts, [], PC[:, 2:3], PB[:, 1:2], 15.0, None, OP.add)
-    V(cp, [], PC[:, 5:6], PB[:, 3:4])
-    V(ts, [], PC[:, 8:9], PB[:, 3:4], -1.0, None, OP.mult)
-    V(ts, [], PC[:, 7:8], T.PI[:], 16.0, None, OP.mult)
-    a = V(ts, [], T.M4[:], T.MI[:, 0:128], 112, None, AND)
-    id16 = V(ts, [], T.ID16[:], T.MI[:, 0:128], PC[:, 6:7], 16.0, OP.is_equal, OP.mult)
-    e8l = V(ts, [a], T.E8L[:], T.M4[0:8, :], PC[0:8, 7:8], None, OP.is_equal)
-    V(ts, [], T.BO[:], T.M4[:], PC[:, 3:4], None, OP.is_equal)
-    V(ts, [], T.K0[:], T.MI[:], PC[:, 2:3], PC[:, 1:2], OP.is_equal, OP.mult)
-    V(ts, [], T.IDH[:], T.MI[:, 0:128], PC[:, 6:7], None, OP.is_equal)
-    V(ts, [], T.CW[:], T.MI[:, 0:4], 2048.0, None, OP.mult)
-    cst = V(ts, [], T.CB[:], T.MI[:, 0:4], 4096.0, None, OP.mult)
+    f = {"allow_small_or_imprecise_dtypes": True}
+    p1 = run("p", g.iota, [], T.TI[:, 0:16], [[-1, 16]], 0, 1)
+    p2 = run("p", g.iota, [], T.TI[:, 16:24], [[-2, 8]], 0, 1)
+    p3 = run("p", g.iota, [], T.N0[:], [[1597, 4], [6388, 48]], -(1 << 23), 0)
+    p4 = run("p", g.iota, [], T.T8[:], [[-16, 8]], 0, 1)
+    p5 = run("p", g.iota, [], T.MI[:], [[1, 128]], 0, -1, **f)
+    p6 = run("p", g.iota, [], T.EI[:], [[16, 8], [0, 16]], 0, -16, **f)
+    p7 = run("p", g.iota, [], T.CW[:], [[2048, 4]], 0, 0, **f)
+    p8 = run("p", g.iota, [], T.CB[:], [[4096, 4]], 0, 0, **f)
 
-    V(ts, [("lsd", 16)], T.SI[:, 0:1], T.SDI[:], 4095, None, AND)
-    a = V(ts, [], T.SI[:, 1:2], T.SDI[:], 12, None, SHR)
-    b = V(cp, [a], T.SF[:, 0:1], T.SI[:, 0:1])
-    V(ts, [], T.SF[:, 1:2], T.SI[:, 1:2], 64.0, -262144.0, OP.mult, OP.add)
-    a = V(ts, [p3, b], T.L0[:], T.N0[:], T.SF[:, 0:1], None, OP.add)
-    tab = V(ts, [("ltab", 32)], T.PW[:, my], T.PW[:, my], PC[:, 0:1], None, OP.add)
-    a = V(ts, [a], T.L[:], T.L0[:], 4095, None, AND)
+    a = V(ts, [p2], T.TA[:], T.TI[:], 15, None, AND)
+    b = V(ts, [], T.PB[:], T.TI[:, 0:1], 1, None, AND)
+    idt = V(ts, [a], T.MOD[:], T.TA[:, 0:16], 0.0, None, OP.is_equal)
+    mw = V(ts, [], T.MW[:], T.TA[:, 16:24], 1.0, None, OP.is_le)
+    b = V(ts, [b], T.PC[:], T.PB[:], -4095.0, 4096.0, OP.mult, OP.add)
+    a = V(cp, [("lsd", 16)], T.SF[:, 0:1], T.SDI[:])
+    d = V(ts, [], T.SI[:], T.SDI[:], 12, None, SHR)
+    l0 = V(ts, [a, p3], T.L0[:], T.N0[:], T.SF[:, 0:1], None, OP.add)
+    tab = V(ts, [("ltab", 32)], T.PW[:, my], T.PW[:, my], -2048.0, None, OP.add)
+
+    a = V(ts, [l0], T.L[:], T.L0[:], 4095, None, AND)
+    V(ts, [d], T.SF[:, 1:2], T.SI[:], 64.0, -262144.0, OP.mult, OP.add)
+    c = V(ts, [p4], T.TS[:], T.T8[:], 4, None, SHR)
+    L64 = T.VB[:, 0:192]
+    l64 = V(ts, [a], L64, T.L[:], 64.0, -262144.0, OP.mult, OP.add)
     rkf = V(cp, [("lrk", 16)], T.RKF[:], T.RKI[:])
-    ll = V(tt, [a], T.LL[:], T.L[:], T.L[:], OP.mult)
-    L64 = T.DA[:, 128:320]
-    V(ts, [], L64, T.L[:], 64.0, -262144.0, OP.mult, OP.add)
-    a = V(ts, [ll], T.TT[:], T.LL[:], T.SF[:, 1:2], None, OP.add)
+    k0 = V(ts, [], T.K0[:], T.N0[:, 0:144], 0.0, None, OP.mult)
+
+    s = A([p5], T.AB[:], T.MI[:], AF.Abs)
+    idn = A([s], T.ID[:], T.AB[:], AF.Relu, bias=1.0, scale=-1.0)
+    id16 = A([idn], T.ID16[:], T.ID[:], AF.Copy, scale=16.0)
+    s = A([p6], T.EA[:], T.EI[:], AF.Abs)
+    ll = A([l64], T.LL[:], L64, AF.Square, bias=4096.0, scale=1.0 / 64)
+    e8l = A([s], T.E8L[:], T.EA[:], AF.Relu, bias=1.0, scale=-1.0)
+    for u in range(EARLY):
+        A([idt], T.DG[:, 128 * u:128 * u + 128], T.ID[:], AF.Copy, scale=T.MOD[:, u:u + 1])
     need("t", [e8l, rkf])
     rt = closed(pe.matmul(T.RQ[:, 0:8], T.E8L[:], T.RKF[:], True, True))
+
+    a = V(ts, [ll], T.TT[:], T.LL[:], T.SF[:, 1:2], None, OP.add)
+    k0 = V(ts, [k0, b, c], T.K0[:, 15:143:16], T.TS[:], 0.0, T.PC[:], OP.is_equal, OP.mult)
     b = V(ts, [a], T.B[:], T.TT[:], 6, 4095, SHR, AND)
     V(ts, [rt], T.A8[:], T.RQ[:, 4:8], 2048.0, None, OP.mult)
+    a8 = V(tt, [p8], T.BP[:], T.RQ[:, 0:4], T.CB[:], OP.add)
     a = V(tt, [b], T.BB[:], T.B[:], T.B[:], OP.mult)
-    a8 = V(tt, [], T.BP[:], T.RQ[:, 0:4], T.CB[:], OP.add)
-    aa = V(tt, [a], T.AA[:], T.BB[:], L64, OP.add)
     V(tt, [a8], T.D1[:], T.A8[:], T.CW[:], OP.subtract)
+    aa = V(tt, [a], T.AA[:], T.BB[:], L64, OP.add)
     dd = V(tt, [], T.D2[:, 0:3], T.CW[:, 1:4], T.A8[:, 0:3], OP.subtract)
     h = V(ts, [aa], T.H[:], T.AA[:, 48:192], 15, 7, SHR, AND)
     w12 = V(ts, [], T.W12[:], T.AA[:, 0:48], 4, 3 << 12, SHR, AND)
-    hb = V(cp, [h], T.HB[:], T.H[:])
+    h16 = V(cp, [h], T.H16[:], T.H[:])
     vv = V(tt, [w12], T.VV[:], T.W12[:], T.B[:, 0:48], OP.add)
-    low = V(ts, [], T.LOW8[:], T.AA[:, 48:192], 4, 255 << 3, SHR, AND)
 
-    for u in range(16):
-        dg = A([idt], T.DG[:, 128 * u:128 * u + 128], T.ID[:], AF.Copy, scale=T.MOD[:, u:u + 1])
     need("t", [("lseen", 16), id16])
     for hf in range(2):
-        o = T.HR[:, 2048 + 512 * hf:2560 + 512 * hf]
+        o = T.HP[:, 512 * hf:512 * hf + 512]
         pe.matmul(o, T.ID[:], T.SEEN[:, 1024 * hf:1024 * hf + 1024:2], True, False)
         c = closed(pe.matmul(o, T.ID16[:], T.SEEN[:, 1024 * hf + 1:1024 * hf + 1024:2], False, True))
         packed = A([c], T.SW[:, 1024 * r + 512 * hf:1024 * r + 512 * hf + 512], o, AF.Copy)
+    mk = [A([h16], T.MK[:, pos(i)], T.MW[:].indirect(T.H16[:, blk(i)]), AF.Copy) for i in range(3)]
+    for u in range(EARLY, 16):
+        dg = A([], T.DG[:, 128 * u:128 * u + 128], T.ID[:], AF.Copy, scale=T.MOD[:, u:u + 1])
 
     Q8 = T.RQ[:, 64:112]
     for w in range(7):
@@ -160,11 +163,6 @@ def rank_program(g, core, T, topo):
         need("t", [c])
         m = pe.matmul(Q8, T.ID[:], o, w == 0, w == 6)
     qt = closed(m)
-    for u in range(16):
-        if u < 8:
-            ev = V(ts, [hb], T.RM[:, u:3 * J:16], T.HB[:], T.MOD[:, u:u + 1], None, OP.mult)
-        else:
-            ea = A([hb], T.RM[:, u:3 * J:16], T.HB[:], AF.Copy, scale=T.MOD[:, u:u + 1])
 
     def send(buf, a0, a1, dests):
         tr = []
@@ -190,81 +188,77 @@ def rank_program(g, core, T, topo):
         g.remote_dma(T.VW[:, w], T.VW[:, w], T.sem.fw, T.sem.lf, pid, rid, bits(on if c < n - 1 else near))
     handed = (n - 1) * len(on) + len(near)
 
-    hr = []
-    for i in range(3):
-        need("t", [ea, ev, cst] + ([packed] if i == 2 else []))
-        pe.matmul(T.HR[:, 1024 * i:1024 * i + 512], T.BO[:], T.RM[:, J * i:J * i + 512], True, True)
-        hr.append(closed(pe.matmul(T.HR[:, 1024 * i + 512:1024 * i + 768], T.BO[:], T.RM[:, J * i + 512:J * i + 768], True, True)))
-    for i in range(3):
-        s = V(tt, [qt, low], T.S[:, blk(i)], T.LOW8[:, blk(i)], Q8, OP.add)
-    V(cp, [], T.QH[:], Q8)
-    e16 = V(ts, [s], T.E16[:], T.S[:], 0.125, None, OP.mult)
-    ee = V(ts, [], T.EE[:], T.AA[:, 48:192], 7, 2047, SHR, AND)
-    V(ts, [], T.BQ[:], T.B[:, 48:192], 8192.0, -2047.0 * 8192.0, OP.mult, OP.add)
-    mk = [V(ts, [hr[0]], T.MK[:, pos(0)], T.HR[:, 0:768], PC[:, 5:6], None, OP.is_equal)]
-    for i in (1, 2):
-        c = A([hr[i]], T.AB[:, pos(i - 1)], T.HR[:, 1024 * i:1024 * i + 768], AF.Abs, bias=PC[:, 8:9])
-        mk.append(A([c], T.MK[:, pos(i)], T.AB[:, pos(i - 1)], AF.Relu, bias=1.0, scale=-1.0))
-    ef = V(ts, [ee], T.EF[:], T.EE[:], 8192.0, None, OP.add)
+    low = V(ts, [], T.LOW8[:], T.AA[:, 48:192], 4, 255 << 3, SHR, AND)
 
-    D = [T.DA[:, 0:48], T.DA[:, 48:96], T.HR[:, 2816:2864]]
+    def offsets(i):
+        return V(tt, [qt, low], T.S[:, blk(i)], T.LOW8[:, blk(i)], Q8, OP.add)
 
-    def look(i):
-        x = V(tt, [("pk", 16), mk[i], e16], T.X1[:, pos(i)], T.PW[:].indirect(T.E16[:, blk(i)]), T.MK[:, pos(i)], OP.mult)
-        need("t", [x])
-        pe.matmul(D[i], T.IDH[:], T.QH[:], True, False)
+    def look(i, e):
+        return V(tt, [("pk", 16), mk[i], e], T.X1[:, pos(i)], T.PW[:].indirect(T.E16[:, blk(i)]), T.MK[:, pos(i)], OP.mult)
+
+    D = [T.DD[:, 0:48], T.DD[:, 48:96], T.DD[:, 512:560]]
+
+    def back(i, x, b):
+        need("t", [x, k0])
         for u in range(16):
-            m = pe.matmul(D[i], T.K0[:, 15 - u:143 - u], T.X1[:, J * i + u:J * i + J:16], False, u == 15)
-        return closed(m)
+            pe.matmul(D[i], T.K0[:, 15 - u:143 - u], T.X1[:, J * i + u:J * i + J:16], u == 0, False)
+        need("t", [b])
+        return closed(pe.matmul(D[i], T.IDN[:], T.BH[:, blk(i)], False, True))
 
-    def resolve(w, o, d):
-        di = V(cp, [d], T.DI[:, w], o)
-        cm = V(tt, [], T.CM[:, w], o, T.BQ[:, w], OP.is_ge)
-        V(ts, [di], T.AL[:, w], T.DI[:, w], 8191, None, AND)
-        mm = V(tt, [cm], T.MM[:, w], T.CM[:, w], T.E8[:, w], OP.mult)
-        return V(tt, [mm], T.CC[:, w], T.AL[:, w], T.MM[:, w], OP.max)
+    offsets(0)
+    c = offsets(1)
+    e = V(ts, [c], T.E16[:, two], T.S[:, two], 0.125, None, OP.mult)
+    x0 = look(0, e)
+    V(ts, [idn], T.IDN[:], T.ID[:], -4096.0, None, OP.mult)
+    bh = V(ts, [], T.BH[:], T.B[:, 48:192], -2048.0, None, OP.add)
+    back(0, x0, bh)
+    x1 = look(1, e)
+    d01 = back(1, x1, bh)
+    c = offsets(2)
+    ee = V(ts, [], T.EE[:], T.AA[:, 48:192], 7, 2047, SHR, AND)
+    e = V(ts, [c], T.E16[:, blk(2)], T.S[:, blk(2)], 0.125, None, OP.mult)
+    x2 = look(2, e)
+    d2 = back(2, x2, bh)
 
-    look(0)
-    for i in range(3):
-        e8 = V(tt, [ef], T.E8[:, blk(i)], T.EF[:, blk(i)], Q8, OP.add)
-    d01 = look(1)
-    d2 = look(2)
-    two = slice(0, 96)
-    need("v", [e8])
-    cc = resolve(two, T.DA[:, two], d01)
-    c = V(ts, [cc], T.S1[:], T.CC[:, two], 8191, 1, AND, SHR)
-    par = V(ts, [], T.PAR[:], T.CC[:, two], 1, None, AND)
-    s16 = V(cp, [c], T.S16[:], T.S1[:])
-    xa = A([s16, ("sn", 16)], T.X2[:, pos(0)], T.SW[:].indirect(T.S16[:, blk(0)]), AF.Copy)
-    xv = V(cp, [s16, ("sn", 16)], T.X2[:, pos(1)], T.SW[:].indirect(T.S16[:, blk(1)]))
-    need("t", [xa, xv, dg])
-    D2 = T.HR[:, two]
+    m = V(tt, [d01, ee], T.M1[:, two], T.EE[:, two], T.DD[:, two], OP.min)
+    c = V(ts, [m], T.C2[:], T.M1[:, two], 2046, None, AND)
+    par = V(ts, [], T.PAR[:], T.M1[:, two], 1, None, AND)
+    V(tt, [c], T.S2[:, blk(0)], T.C2[:, blk(0)], Q8, OP.add)
+    c = V(tt, [], T.S2[:, blk(1)], T.C2[:, blk(1)], Q8, OP.add)
+    s16 = V(ts, [c], T.S16[:], T.S2[:], 0.5, None, OP.mult)
+    ha = A([s16, ("sn", 16)], T.X2[:, pos(0)], T.SW[:].indirect(T.S16[:, blk(0)]), AF.Copy)
+    hv = V(cp, [s16, ("sn", 16)], T.X2[:, pos(1)], T.SW[:].indirect(T.S16[:, blk(1)]))
+    need("t", [ha, hv, dg])
+    HU = T.HU[:, two]
     for u in range(16):
-        m = pe.matmul(D2, T.DG[:, 128 * u:128 * u + 128], T.X2[:, u:2 * J:16], u == 0, u == 15)
+        m = pe.matmul(HU, T.DG[:, 128 * u:128 * u + 128], T.X2[:, u:2 * J:16], u == 0, u == 15)
     kn = closed(m)
-    V(ts, [], T.GP[:, blk(0)], T.CC[:, blk(0)], 65536.0 + 16384.0, None, OP.add)
-    V(ts, [], T.GP[:, blk(1)], T.CC[:, blk(1)], 65536.0, None, OP.add)
+
+    QM, GP, M2 = T.VB[:, 192:336], T.VB[:, 336:480], T.VB[:, 0:48]
+    for i, k in enumerate((65536.0 + 16384.0, 65536.0, 32768.0)):
+        qm = V(ts, [], T.VB[:, 192 + 48 * i:240 + 48 * i], Q8, k, None, OP.add)
     pp = V(ts, [par], T.PP[:], T.PAR[:], float(-15 * (65536 >> (r + 4))), float(65536 >> r), OP.mult, OP.add)
-    cc = resolve(blk(2), D[2], d2)
-    g2 = V(ts, [cc], T.GP[:, blk(2)], T.CC[:, blk(2)], 32768.0, None, OP.add)
-    t = V(tt, [kn, pp], T.TK[:], D2, T.PP[:], OP.mult)
+    m = V(tt, [d2], T.M1[:, blk(2)], T.EE[:, blk(2)], D[2], OP.min)
+    c = V(ts, [m], T.C1[:], T.M1[:], 2047, None, AND)
+    gp = V(tt, [c, qm], GP, T.C1[:], QM, OP.add)
+    t = V(tt, [kn, pp], T.TK[:], HU, T.PP[:], OP.mult)
     t = V(ts, [t], T.KB[:], T.TK[:], 65536, None, AND)
-    t = V(tt, [t], T.VAL[:], T.GP[:, two], T.KB[:], OP.subtract)
-    t = V(tt, [t, g2], T.MX[:, blk(0)], T.VAL[:, blk(0)], T.VAL[:, blk(1)], OP.max)
-    t = V(tt, [t], T.MX[:, blk(1)], T.MX[:, blk(0)], T.GP[:, blk(2)], OP.max)
-    t = V(ts, [t], T.XG[:], T.MX[:, blk(1)], 8191, None, AND)
+    t = V(tt, [t, gp], T.VAL[:], T.VB[:, 336:432], T.KB[:], OP.subtract)
+    t = V(tt, [t], M2, T.VAL[:, blk(1)], T.VB[:, 432:480], OP.max)
+    t = V(tt, [t], T.MX[:], T.VAL[:, blk(0)], M2, OP.max)
+    t = V(ts, [t], T.XG[:], T.MX[:], 8191, None, AND)
     t = V(cp, [t], T.X16[:], T.XG[:])
 
     here = [("lvec", 16), ("vp", n * len(on))] + [("x%d" % c, len(off)) for c in range(n)] + [("fw", handed)]
-    ya = A(here + [t], T.Y[:, 384:768], T.VW[:].indirect(T.X16[:, 24:48]), AF.Copy)
+    ya = A(here + [t], T.Y[:, 16 * YV:768], T.VW[:].indirect(T.X16[:, YV:48]), AF.Copy)
     ch = V(cp, [], T.CH[:], T.XG[:])
-    yv = V(cp, here + [t], T.Y[:, 0:384], T.VW[:].indirect(T.X16[:, 0:24]))
+    yv = V(cp, here + [t], T.Y[:, 0:16 * YV], T.VW[:].indirect(T.X16[:, 0:YV]))
     need("s", [ch])
     g.sync.dma_start(T.chosen[:], T.CH[:]).then_inc(T.sem.st, 16)
     need("a", [ya])
-    act.dma_start(T.y[:, 384:768], T.Y[:, 384:768]).then_inc(T.sem.st, 16)
+    act.dma_start(T.y[:, 16 * YV:768], T.Y[:, 16 * YV:768]).then_inc(T.sem.st, 16)
     need("s", [yv])
-    g.sync.dma_start(T.y[:, 0:384], T.Y[:, 0:384]).then_inc(T.sem.st, 16)
+    g.sync.dma_start(T.y[:, 0:16 * YV], T.Y[:, 0:16 * YV]).then_inc(T.sem.st, 16)
 
     need("p", [(q, cnt[q]) for q in ("v", "a", "t", "p")])
     need("p", [("ls", (2 + n) * 16), ("lf", handed), ("vp", n * len(on)), ("fw", handed), ("pk", 16), ("sn", 16), ("st", 48)])

@@ -4,30 +4,40 @@ from concourse.mybir import AluOpType as OP, ActivationFunctionType as AF
 M, K, N = 2048, 48, 4
 J = 16 * K
 CUTS = (0, 896, 1536, 2048)
-YV = 22
-EARLY = 3
+YV = 24
+HV = 24
+LOOKS = (((0, 48),), ((0, 48),), ((0, 24), (24, 48)))
+ORDER = {
+    "p": "pu n0 cp n1 ei cb p8",
+    "v": "TM TA PB sf ID MOD s0 tab s1 l0 si MW l1 m0 ra sg m1 E8 KZ r1 t0 r0 r2 t1 b0 b1 c0 c1 a0 a1 TS W H VV PC HH "
+         "u0 u1 u2 u3 u4 u5 u6 K0 LO o2 o1 o0 BH E16 IDN EE x00 x10 x20 M0 C0 S0 L0 P0 M1 x21 C1 F0 S1 L1 G0 hv P1 M2 C2 G1 S2 "
+         "e1 e2 F1 TK KB f1 KK f3 f2 X X16 yv",
+    "a": "d9 d14 d12 d1 d13 i6 cw d2 q0 q1 d11 d7 d0 d8 sw0 d15 sw1 k0 k1 k2 d3 d6 d4 d10 d5 h0 ha ya",
+    "t": " ".join(["pe0 po0 pe1 po1 rt"] + ["Q%d" % w for w in range(7)]
+                  + [" ".join(["y%d_%d" % (i, u) for u in range(16)] + ["Y%d" % i]) for i in range(3)] + ["z%d" % u for u in range(16)])}
 
 I4, F4, F2, H2, U2 = "int32", "float32", "bfloat16", "float16", "uint16"
 SCRATCH = {n: ("sbuf", [p, c], d) for n, p, c, d in (
     ("PW", 128, 1024, I4), ("SW", 128, 4096, F2), ("VW", 128, 8192, F2), ("SEEN", 128, 2048, F2), ("SDI", 128, 1, I4),
-    ("RKI", 8, 8, I4), ("RKF", 8, 8, F4), ("TI", 128, 24, I4), ("TA", 128, 24, I4), ("T8", 128, 8, I4), ("TS", 128, 8, I4),
-    ("MI", 128, 128, F4), ("AB", 128, 128, F2), ("N0", 128, 192, I4), ("EI", 8, 128, F4), ("EA", 8, 128, F4), ("PB", 128, 1, I4),
+    ("RKI", 8, 8, I4), ("RKA", 8, 4, F4), ("RT", 8, 11, F4), ("TI", 128, 16, I4), ("TA", 128, 24, I4), ("T8", 128, 8, I4),
+    ("TS", 128, 8, I4), ("MI", 128, 128, F4), ("N0", 128, 192, I4), ("EI", 8, 128, F4), ("PB", 128, 1, I4),
     ("PC", 128, 1, F4), ("K0", 128, 144, H2), ("ID", 128, 128, F2), ("ID16", 128, 128, F2), ("IDN", 128, 128, H2),
     ("E8L", 8, 128, F4), ("MOD", 128, 16, F4), ("MW", 128, 8, F2), ("DG", 128, 2048, F2), ("SI", 128, 1, I4), ("SF", 128, 2, F4),
     ("L0", 128, 192, I4), ("L", 128, 192, I4), ("LL", 128, 192, F4), ("TT", 128, 192, I4), ("B", 128, 192, I4),
     ("BB", 128, 192, I4), ("AA", 128, 192, I4), ("H", 128, 144, I4), ("H16", 128, 144, U2), ("W12", 128, 48, I4),
-    ("VV", 128, 48, I4), ("TM", 128, 336, F2), ("CW", 128, 4, F4), ("CB", 128, 4, F4), ("A8", 128, 4, F4), ("BP", 128, 4, F4),
-    ("D1", 128, 4, F4), ("D2", 128, 4, F4), ("LOW8", 128, 144, I4), ("EE", 128, 144, I4), ("BH", 128, 144, H2),
+    ("VV", 128, 48, I4), ("TM", 128, 336, F2), ("CW", 8, 4, F4), ("CB", 8, 4, F4),
+    ("LOW8", 128, 144, I4), ("EE", 128, 144, I4), ("BH", 128, 144, H2),
     ("S", 128, 144, I4), ("E16", 128, 144, U2), ("MK", 128, 2304, F2), ("X1", 128, 2304, H2), ("X2", 128, 1536, F2),
-    ("M1", 128, 144, I4), ("C1", 128, 144, I4), ("C2", 128, 96, I4), ("S2", 128, 96, I4), ("S16", 128, 96, U2), ("PAR", 128, 96, I4),
-    ("PP", 128, 96, I4), ("TK", 128, 96, I4), ("KB", 128, 96, I4), ("VAL", 128, 96, F4), ("MX", 128, 48, I4), ("XG", 128, 48, I4),
-    ("X16", 128, 48, U2), ("CH", 128, 48, F4), ("Y", 128, 768, F2))}
+    ("M1", 128, 144, I4), ("C2", 128, 144, I4), ("S2", 128, 144, I4), ("S16", 128, 96, U2), ("PAR", 128, 96, I4), ("G", 128, 144, I4),
+    ("PP", 128, 96, I4), ("TK", 128, 96, I4), ("KK", 128, 48, F4), ("KB", 128, 96, I4), ("X", 128, 48, F4), ("W", 128, 48, F4),
+    ("X16", 128, 48, U2), ("Y", 128, 768, F2))}
 SCRATCH["HP"] = ("psum", [128, 1024], F4)
 SCRATCH["HU"] = ("psum", [128, 512], F4)
 SCRATCH["DD"] = ("psum", [128, 1024], F4)
 SCRATCH["RQ"] = ("psum", [128, 512], F4)
 SCRATCH["VB"] = ("psum", [128, 512], F4)
-SEMAPHORES = ["v", "a", "t", "p", "lsd", "ltab", "lrk", "lseen", "lvec", "pk", "sn", "vp", "x0", "x1", "x2", "fw", "ls", "lf", "st"]
+SEMAPHORES = ["v", "a", "t", "p", "lsd", "ltab", "lrk", "ls0", "ls1", "lvec", "pk", "sn", "vp", "s0", "s1", "fs", "x0", "x1", "x2", "fw",
+              "ls", "lf", "st"]
 
 
 def rank_program(g, core, T, topo):
@@ -45,221 +55,206 @@ def rank_program(g, core, T, topo):
     half = len(off) // 2
     lanes = {partner: bits(on), cross: bits(off[:half]), diag: bits(off[half:])}
     vec, act, pe = g.vector, g.scalar, g.tensor
-    cnt = {"v": 0, "a": 0, "t": 0, "p": 0}
-    lvl = {"v": {}, "a": {}, "t": {}, "p": {}, "s": {}}
     eng = {"v": vec, "a": act, "t": pe, "p": g, "s": g.sync}
+    place = {name: (q, i + 1) for q in ORDER for i, name in enumerate(ORDER[q].split())}
+    todo = {}
+    lvl = {q: {} for q in eng}
 
     def need(q, deps):
-        for s, n in deps:
+        for d in deps:
+            s, n = place[d] if d in place else d
             if lvl[q].get(s, 0) < n:
                 eng[q].wait_ge(T.sem[s], n)
                 lvl[q][s] = n
 
-    def run(q, call, deps, *args, **kw):
-        need(q, deps)
-        call(*args, **kw).then_inc(T.sem[q], 1)
-        cnt[q] += 1
-        return (q, cnt[q])
-
-    def V(call, deps, *args):
-        return run("v", call, deps, *args)
-
-    def A(deps, *args, **kw):
-        return run("a", act.activation, deps, *args, **kw)
-
-    def closed(m):
-        m.then_inc(T.sem.t, 1)
-        cnt["t"] += 1
-        return ("t", cnt["t"])
+    def call(name, deps, f, *args, **kw):
+        todo[name] = (deps, f, args, kw)
 
     def blk(i):
         return slice(48 * i, 48 * i + 48)
 
-    def pos(i):
-        return slice(J * i, J * i + J)
+    def pos(i, a=0, b=48):
+        return slice(J * i + 16 * a, J * i + 16 * b)
 
-    ts, tt, cp = vec.tensor_scalar, vec.tensor_tensor, vec.tensor_copy
+    ts, tt, cp, copy, mm = vec.tensor_scalar, vec.tensor_tensor, vec.tensor_copy, act.activation, pe.matmul
     SHR, AND = OP.arith_shift_right, OP.bitwise_and
-    two = slice(0, 96)
+    two, last = slice(0, 96), slice(48, 192)
+    halves = (slice(0, 96), slice(96, 192))
 
     my = slice(256 * r, 256 * r + 256)
     g.sync.dma_start(T.SDI[:], T.sd[:]).then_inc(T.sem.lsd, 16)
     act.dma_start(T.PW[1:128:2, my], T.ali[:]).then_inc(T.sem.ltab, 16)
     g.sync.dma_start(T.PW[0:128:2, my], T.thr[:]).then_inc(T.sem.ltab, 16)
     act.dma_start(T.RKI[:], T.rk[:]).then_inc(T.sem.lrk, 16)
-    g.sync.dma_start(T.SEEN[:], T.seen[:]).then_inc(T.sem.lseen, 16)
+    for h in range(2):
+        w = slice(1024 * h, 1024 * h + 1024)
+        g.sync.dma_start(T.SEEN[:, w], T.seen[:, w]).then_inc(T.sem["ls%d" % h], 16)
     g.sync.dma_start(T.VW[:, M * r:M * r + M], T.vec[:]).then_inc(T.sem.lvec, 16)
 
     f = {"allow_small_or_imprecise_dtypes": True}
-    p1 = run("p", g.iota, [], T.TI[:, 0:16], [[-1, 16]], 0, 1)
-    p2 = run("p", g.iota, [], T.TI[:, 16:24], [[-2, 8]], 0, 1)
-    p3 = run("p", g.iota, [], T.N0[:], [[1597, 4], [6388, 48]], -(1 << 23), 0)
-    p4 = run("p", g.iota, [], T.T8[:], [[-16, 8]], 0, 1)
-    p5 = run("p", g.iota, [], T.MI[:], [[1, 128]], 0, -1, **f)
-    p6 = run("p", g.iota, [], T.EI[:], [[16, 8], [0, 16]], 0, -16, **f)
-    p7 = run("p", g.iota, [], T.CW[:], [[2048, 4]], 0, 0, **f)
-    p8 = run("p", g.iota, [], T.CB[:], [[4096, 4]], 0, 0, **f)
 
-    a = V(ts, [p2], T.TA[:], T.TI[:], 15, None, AND)
-    b = V(ts, [], T.PB[:], T.TI[:, 0:1], 1, None, AND)
-    idt = V(ts, [a], T.MOD[:], T.TA[:, 0:16], 0.0, None, OP.is_equal)
-    mw = V(ts, [], T.MW[:], T.TA[:, 16:24], 1.0, None, OP.is_le)
-    b = V(ts, [b], T.PC[:], T.PB[:], -4095.0, 4096.0, OP.mult, OP.add)
-    a = V(cp, [("lsd", 16)], T.SF[:, 0:1], T.SDI[:])
-    d = V(ts, [], T.SI[:], T.SDI[:], 12, None, SHR)
-    l0 = V(ts, [a, p3], T.L0[:], T.N0[:], T.SF[:, 0:1], None, OP.add)
-    tab = V(ts, [("ltab", 32)], T.PW[:, my], T.PW[:, my], -2048.0, None, OP.add)
-
-    a = V(ts, [l0], T.L[:], T.L0[:], 4095, None, AND)
-    V(ts, [d], T.SF[:, 1:2], T.SI[:], 64.0, -262144.0, OP.mult, OP.add)
-    c = V(ts, [p4], T.TS[:], T.T8[:], 4, None, SHR)
-    L64 = T.VB[:, 0:192]
-    l64 = V(ts, [a], L64, T.L[:], 64.0, -262144.0, OP.mult, OP.add)
-    rkf = V(cp, [("lrk", 16)], T.RKF[:], T.RKI[:])
-    k0 = V(ts, [], T.K0[:], T.N0[:, 0:144], 0.0, None, OP.mult)
-
-    s = A([p5], T.AB[:], T.MI[:], AF.Abs)
-    idn = A([s], T.ID[:], T.AB[:], AF.Relu, bias=1.0, scale=-1.0)
-    id16 = A([idn], T.ID16[:], T.ID[:], AF.Copy, scale=16.0)
-    s = A([p6], T.EA[:], T.EI[:], AF.Abs)
-    ll = A([l64], T.LL[:], L64, AF.Square, bias=4096.0, scale=1.0 / 64)
-    e8l = A([s], T.E8L[:], T.EA[:], AF.Relu, bias=1.0, scale=-1.0)
-    for u in range(EARLY):
-        A([idt], T.DG[:, 128 * u:128 * u + 128], T.ID[:], AF.Copy, scale=T.MOD[:, u:u + 1])
-    need("t", [e8l, rkf])
-    rt = closed(pe.matmul(T.RQ[:, 0:8], T.E8L[:], T.RKF[:], True, True))
-
-    a = V(ts, [ll], T.TT[:], T.LL[:], T.SF[:, 1:2], None, OP.add)
-    k0 = V(ts, [k0, b, c], T.K0[:, 15:143:16], T.TS[:], 0.0, T.PC[:], OP.is_equal, OP.mult)
-    b = V(ts, [a], T.B[:], T.TT[:], 6, 4095, SHR, AND)
-    V(ts, [rt], T.A8[:], T.RQ[:, 4:8], 2048.0, None, OP.mult)
-    a8 = V(tt, [p8], T.BP[:], T.RQ[:, 0:4], T.CB[:], OP.add)
-    a = V(tt, [b], T.BB[:], T.B[:], T.B[:], OP.mult)
-    V(tt, [a8], T.D1[:], T.A8[:], T.CW[:], OP.subtract)
-    aa = V(tt, [a], T.AA[:], T.BB[:], L64, OP.add)
-    dd = V(tt, [], T.D2[:, 0:3], T.CW[:, 1:4], T.A8[:, 0:3], OP.subtract)
-    h = V(ts, [aa], T.H[:], T.AA[:, 48:192], 15, 7, SHR, AND)
-    w12 = V(ts, [], T.W12[:], T.AA[:, 0:48], 4, 3 << 12, SHR, AND)
-    h16 = V(cp, [h], T.H16[:], T.H[:])
-    vv = V(tt, [w12], T.VV[:], T.W12[:], T.B[:, 0:48], OP.add)
-
-    need("t", [("lseen", 16), id16])
-    for hf in range(2):
-        o = T.HP[:, 512 * hf:512 * hf + 512]
-        pe.matmul(o, T.ID[:], T.SEEN[:, 1024 * hf:1024 * hf + 1024:2], True, False)
-        c = closed(pe.matmul(o, T.ID16[:], T.SEEN[:, 1024 * hf + 1:1024 * hf + 1024:2], False, True))
-        packed = A([c], T.SW[:, 1024 * r + 512 * hf:1024 * r + 512 * hf + 512], o, AF.Copy)
-    mk = [A([h16], T.MK[:, pos(i)], T.MW[:].indirect(T.H16[:, blk(i)]), AF.Copy) for i in range(3)]
-    for u in range(EARLY, 16):
-        dg = A([], T.DG[:, 128 * u:128 * u + 128], T.ID[:], AF.Copy, scale=T.MOD[:, u:u + 1])
-
-    Q8 = T.RQ[:, 64:112]
-    for w in range(7):
-        o = T.TM[:, 48 * w:48 * w + 48]
-        if w < 4:
-            c = V(ts, [vv, dd], o, T.VV[:], T.BP[:, w:w + 1], T.D1[:, w:w + 1], OP.is_ge, OP.mult)
-        else:
-            c = V(ts, [], o, T.VV[:], 4096.0 * (w - 3), T.D2[:, w - 4:w - 3], OP.is_ge, OP.mult)
-        need("t", [c])
-        m = pe.matmul(Q8, T.ID[:], o, w == 0, w == 6)
-    qt = closed(m)
+    def ramp(*args, **kw):
+        g.iota(*args, **kw).then_inc(T.sem.p, 1)
 
     def send(buf, a0, a1, dests):
         tr = []
-        for d, mask, sem in dests:
+        for d, mask, s in dests:
             rid, pid = topo.addr(d, core)
-            tr.append(RemoteDMATransfer(dst_ids=[DstId(rid=rid, pnc=pid)], dma_engine_mask=mask, remote_sem=T.sem[sem],
+            tr.append(RemoteDMATransfer(dst_ids=[DstId(rid=rid, pnc=pid)], dma_engine_mask=mask, remote_sem=T.sem[s],
                                         srcs=[T[buf][:, a0:a1]], dsts=[T[buf][:, a0:a1]]))
         g.remote_dma_fused(tr, local_sem=T.sem.ls)
 
-    need("p", [tab])
+    def hand(buf, a0, a1, s, es):
+        rid, pid = topo.addr(partner, core)
+        g.remote_dma(T[buf][:, a0:a1], T[buf][:, a0:a1], T.sem[s], T.sem.lf, pid, rid, bits(es))
+
+    ramp(T.TI[:, 0:16], [[-1, 16]], 0, 1)
+    ramp(T.N0[:, 0:96], [[1597, 2], [6388, 48]], -(1 << 23), 0)
+    ramp(T.MI[:], [[1, 128]], 0, -1, **f)
+    ramp(T.N0[:, 96:192], [[1597, 2], [6388, 48]], 2 * 1597 - (1 << 23), 0)
+    ramp(T.EI[:], [[16, 8], [0, 16]], 0, -16, **f)
+    ramp(T.CB[:], [[4096, 4]], 0, 0, **f)
+    far = T.rank_of(cross)
+    need("p", ["tab"])
     send("PW", 256 * r, 256 * r + 256, [(d, lanes[d], "pk") for d in (cross, diag, partner)])
-    need("p", [packed])
-    send("SW", 1024 * r, 1024 * r + 1024, [(d, lanes[d], "sn") for d in (cross, diag, partner)])
+    ramp(T.T8[:], [[-16, 8]], 0, 1)
+    for h in range(2):
+        need("p", ["sw%d" % h])
+        o = 1024 * r + 512 * h
+        send("SW", o, o + 512, [(cross, bits(off), "s%d" % h), (partner, bits(on), "sn")])
     need("p", [("lvec", 16)])
     pieces = list(zip(CUTS, CUTS[1:]))
     n = len(pieces)
     for c, (a0, a1) in enumerate(pieces):
-        send("VW", M * r + a0, M * r + a1, [(cross, bits(off), "x%d" % c), (partner, bits(on), "vp")])
-    rid, pid = topo.addr(partner, core)
+        send("VW", M * r + a0, M * r + a1, [(cross, bits(off), "x%d" % c)])
+    for h in range(2):
+        need("p", [("s%d" % h, len(off))])
+        o = 1024 * far + 512 * h
+        hand("SW", o, o + 512, "fs", on)
+    send("VW", M * r, M * r + M, [(partner, bits(on), "vp")])
     for c, (a0, a1) in enumerate(pieces):
         need("p", [("x%d" % c, len(off))])
-        w = slice(M * T.rank_of(cross) + a0, M * T.rank_of(cross) + a1)
-        g.remote_dma(T.VW[:, w], T.VW[:, w], T.sem.fw, T.sem.lf, pid, rid, bits(on if c < n - 1 else near))
-    handed = (n - 1) * len(on) + len(near)
+        hand("VW", M * far + a0, M * far + a1, "fw", near)
+    hs, handed = 2 * len(on), n * len(near)
 
-    low = V(ts, [], T.LOW8[:], T.AA[:, 48:192], 4, 255 << 3, SHR, AND)
-
-    def offsets(i):
-        return V(tt, [qt, low], T.S[:, blk(i)], T.LOW8[:, blk(i)], Q8, OP.add)
-
-    def look(i, e):
-        return V(tt, [("pk", 16), mk[i], e], T.X1[:, pos(i)], T.PW[:].indirect(T.E16[:, blk(i)]), T.MK[:, pos(i)], OP.mult)
-
-    D = [T.DD[:, 0:48], T.DD[:, 48:96], T.DD[:, 512:560]]
-
-    def back(i, x, b):
-        need("t", [x, k0])
-        for u in range(16):
-            pe.matmul(D[i], T.K0[:, 15 - u:143 - u], T.X1[:, J * i + u:J * i + J:16], u == 0, False)
-        need("t", [b])
-        return closed(pe.matmul(D[i], T.IDN[:], T.BH[:, blk(i)], False, True))
-
-    offsets(0)
-    c = offsets(1)
-    e = V(ts, [c], T.E16[:, two], T.S[:, two], 0.125, None, OP.mult)
-    x0 = look(0, e)
-    V(ts, [idn], T.IDN[:], T.ID[:], -4096.0, None, OP.mult)
-    bh = V(ts, [], T.BH[:], T.B[:, 48:192], -2048.0, None, OP.add)
-    back(0, x0, bh)
-    x1 = look(1, e)
-    d01 = back(1, x1, bh)
-    c = offsets(2)
-    ee = V(ts, [], T.EE[:], T.AA[:, 48:192], 7, 2047, SHR, AND)
-    e = V(ts, [c], T.E16[:, blk(2)], T.S[:, blk(2)], 0.125, None, OP.mult)
-    x2 = look(2, e)
-    d2 = back(2, x2, bh)
-
-    m = V(tt, [d01, ee], T.M1[:, two], T.EE[:, two], T.DD[:, two], OP.min)
-    c = V(ts, [m], T.C2[:], T.M1[:, two], 2046, None, AND)
-    par = V(ts, [], T.PAR[:], T.M1[:, two], 1, None, AND)
-    V(tt, [c], T.S2[:, blk(0)], T.C2[:, blk(0)], Q8, OP.add)
-    c = V(tt, [], T.S2[:, blk(1)], T.C2[:, blk(1)], Q8, OP.add)
-    s16 = V(ts, [c], T.S16[:], T.S2[:], 0.5, None, OP.mult)
-    ha = A([s16, ("sn", 16)], T.X2[:, pos(0)], T.SW[:].indirect(T.S16[:, blk(0)]), AF.Copy)
-    hv = V(cp, [s16, ("sn", 16)], T.X2[:, pos(1)], T.SW[:].indirect(T.S16[:, blk(1)]))
-    need("t", [ha, hv, dg])
-    HU = T.HU[:, two]
+    call("TA", ["pu"], ts, T.TA[:, 0:16], T.TI[:, 0:16], 15, None, AND)
+    call("MOD", ["TA"], ts, T.MOD[:], T.TA[:, 0:16], 0.0, None, OP.is_equal)
+    call("PB", ["pu"], ts, T.PB[:], T.TI[:, 0:1], 1, None, AND)
+    call("PC", ["PB"], ts, T.PC[:], T.PB[:], -4095.0, 4096.0, OP.mult, OP.add)
+    call("TM", ["pu"], ts, T.TA[:, 16:24], T.TI[:, 0:16:2], 15, None, AND)
+    call("MW", ["TM"], ts, T.MW[:], T.TA[:, 16:24], 1.0, None, OP.is_le)
+    call("ID", ["cp"], ts, T.ID[:], T.MI[:], 0.0, None, OP.is_equal)
+    call("IDN", ["ID"], ts, T.IDN[:], T.ID[:], -4096.0, None, OP.mult)
+    call("KZ", ["n0", "n1"], ts, T.K0[:], T.N0[:, 0:144], 0.0, None, OP.mult)
+    call("TS", ["p8"], ts, T.TS[:], T.T8[:], 4, None, SHR)
+    call("K0", ["KZ", "TS", "PC"], ts, T.K0[:, 15:143:16], T.TS[:], 0.0, T.PC[:], OP.is_equal, OP.mult)
+    call("E8", ["ei"], ts, T.E8L[:], T.EI[:], 0.0, None, OP.is_equal)
+    call("i6", ["ID"], copy, T.ID16[:], T.ID[:], AF.Copy, scale=16.0)
     for u in range(16):
-        m = pe.matmul(HU, T.DG[:, 128 * u:128 * u + 128], T.X2[:, u:2 * J:16], u == 0, u == 15)
-    kn = closed(m)
+        call("d%d" % u, ["ID", "MOD"], copy, T.DG[:, 128 * u:128 * u + 128], T.ID[:], AF.Copy, scale=T.MOD[:, u:u + 1])
 
-    QM, GP, M2 = T.VB[:, 192:336], T.VB[:, 336:480], T.VB[:, 0:48]
-    for i, k in enumerate((65536.0 + 16384.0, 65536.0, 32768.0)):
-        qm = V(ts, [], T.VB[:, 192 + 48 * i:240 + 48 * i], Q8, k, None, OP.add)
-    pp = V(ts, [par], T.PP[:], T.PAR[:], float(-15 * (65536 >> (r + 4))), float(65536 >> r), OP.mult, OP.add)
-    m = V(tt, [d2], T.M1[:, blk(2)], T.EE[:, blk(2)], D[2], OP.min)
-    c = V(ts, [m], T.C1[:], T.M1[:], 2047, None, AND)
-    gp = V(tt, [c, qm], GP, T.C1[:], QM, OP.add)
-    t = V(tt, [kn, pp], T.TK[:], HU, T.PP[:], OP.mult)
-    t = V(ts, [t], T.KB[:], T.TK[:], 65536, None, AND)
-    t = V(tt, [t, gp], T.VAL[:], T.VB[:, 336:432], T.KB[:], OP.subtract)
-    t = V(tt, [t], M2, T.VAL[:, blk(1)], T.VB[:, 432:480], OP.max)
-    t = V(tt, [t], T.MX[:], T.VAL[:, blk(0)], M2, OP.max)
-    t = V(ts, [t], T.XG[:], T.MX[:], 8191, None, AND)
-    t = V(cp, [t], T.X16[:], T.XG[:])
+    call("tab", [("ltab", 32)], ts, T.PW[:, my], T.PW[:, my], -2048.0, None, OP.add)
+    for h in range(2):
+        o, c = T.HP[:, 512 * h:512 * h + 512], 1024 * h
+        call("pe%d" % h, ["ID", ("ls%d" % h, 16)], mm, o, T.ID[:], T.SEEN[:, c:c + 1024:2], True, False)
+        call("po%d" % h, ["i6", ("ls%d" % h, 16)], mm, o, T.ID16[:], T.SEEN[:, c + 1:c + 1024:2], False, True)
+        call("sw%d" % h, ["po%d" % h], copy, T.SW[:, 1024 * r + 512 * h:1024 * r + 512 * h + 512], o, AF.Copy)
+    call("cw", ["cb"], copy, T.CW[:], T.CB[:], AF.Copy, scale=0.5)
+    call("ra", [("lrk", 16)], ts, T.RKA[:], T.RKI[:, 4:8], 2048.0, None, OP.mult)
+    call("r0", [("lrk", 16), "cb"], tt, T.RT[:, 0:4], T.RKI[:, 0:4], T.CB[:], OP.add)
+    call("r1", ["ra", "cw"], tt, T.RT[:, 4:8], T.RKA[:], T.CW[:], OP.subtract)
+    call("r2", ["ra", "cw"], tt, T.RT[:, 8:11], T.CW[:, 1:4], T.RKA[:, 0:3], OP.subtract)
+    call("rt", ["E8", "r0", "r1", "r2"], mm, T.DD[:, 960:971], T.E8L[:], T.RT[:], True, True)
 
-    here = [("lvec", 16), ("vp", n * len(on))] + [("x%d" % c, len(off)) for c in range(n)] + [("fw", handed)]
-    ya = A(here + [t], T.Y[:, 16 * YV:768], T.VW[:].indirect(T.X16[:, YV:48]), AF.Copy)
-    ch = V(cp, [], T.CH[:], T.XG[:])
-    yv = V(cp, here + [t], T.Y[:, 0:16 * YV], T.VW[:].indirect(T.X16[:, 0:YV]))
-    need("s", [ch])
-    g.sync.dma_start(T.chosen[:], T.CH[:]).then_inc(T.sem.st, 16)
-    need("a", [ya])
+    call("sf", [("lsd", 16)], cp, T.SF[:, 0:1], T.SDI[:])
+    call("si", [("lsd", 16)], ts, T.SI[:], T.SDI[:], 12, None, SHR)
+    call("sg", ["si"], ts, T.SF[:, 1:2], T.SI[:], 64.0, -262144.0, OP.mult, OP.add)
+    for h, w in enumerate(halves):
+        l64 = (T.VB[:, 0:96], T.HU[:, 256:352])[h]
+        i = lambda s: s + str(h)
+        call(i("s"), ["sf", i("n")], ts, T.L0[:, w], T.N0[:, w], T.SF[:, 0:1], None, OP.add)
+        call(i("l"), [i("s")], ts, T.L[:, w], T.L0[:, w], 4095, None, AND)
+        call(i("m"), [i("l")], ts, l64, T.L[:, w], 64.0, -262144.0, OP.mult, OP.add)
+        call(i("q"), [i("m")], copy, T.LL[:, w], l64, AF.Square, bias=4096.0, scale=1.0 / 64)
+        call(i("t"), [i("q"), "sg"], ts, T.TT[:, w], T.LL[:, w], T.SF[:, 1:2], None, OP.add)
+        call(i("b"), [i("t")], ts, T.B[:, w], T.TT[:, w], 6, 4095, SHR, AND)
+        call(i("c"), [i("b")], tt, T.BB[:, w], T.B[:, w], T.B[:, w], OP.mult)
+        call(i("a"), [i("c")], tt, T.AA[:, w], T.BB[:, w], l64, OP.add)
+    call("H", ["a0", "a1"], ts, T.H[:], T.AA[:, last], 15, 7, SHR, AND)
+    call("HH", ["H"], cp, T.H16[:], T.H[:])
+    call("LO", ["a0", "a1"], ts, T.LOW8[:], T.AA[:, last], 4, 255 << 3, SHR, AND)
+    call("EE", ["a0", "a1"], ts, T.EE[:], T.AA[:, last], 7, 2047, SHR, AND)
+    call("BH", ["b0", "b1"], ts, T.BH[:], T.B[:, last], -2048.0, None, OP.add)
+
+    Q8 = T.RQ[:, 0:48]
+    call("W", ["a0"], ts, T.W12[:], T.AA[:, 0:48], 4, 3 << 12, SHR, AND)
+    call("VV", ["W", "b0"], tt, T.VV[:], T.W12[:], T.B[:, 0:48], OP.add)
+    for w in range(7):
+        lim = T.DD[:, 960 + w:961 + w] if w < 4 else 4096.0 * (w - 3)
+        call("u%d" % w, ["VV", "rt"], ts, T.TM[:, blk(w)], T.VV[:], lim, T.DD[:, 964 + w:965 + w], OP.is_ge, OP.mult)
+        call("Q%d" % w, ["ID", "u%d" % w], mm, Q8, T.ID[:], T.TM[:, blk(w)], w == 0, w == 6)
+
+    D = [T.DD[:, 0:48], T.DD[:, 512:560], T.DD[:, 48:96]]
+    for i in range(3):
+        call("o%d" % i, ["Q6", "LO"], tt, T.S[:, blk(i)], T.LOW8[:, blk(i)], Q8, OP.add)
+        call("k%d" % i, ["HH", "MW"], copy, T.MK[:, pos(i)], T.MW[:].indirect(T.H16[:, blk(i)]), AF.Copy)
+        for c, (a, b) in enumerate(LOOKS[i]):
+            call("x%d%d" % (i, c), [("pk", 16), "tab", "k%d" % i, "E16"], tt, T.X1[:, pos(i, a, b)],
+                 T.PW[:].indirect(T.E16[:, 48 * i + a:48 * i + b]), T.MK[:, pos(i, a, b)], OP.mult)
+        done = ["x%d%d" % (i, c) for c in range(len(LOOKS[i]))]
+        for u in range(16):
+            call("y%d_%d" % (i, u), done + ["K0"] + (["M0"] if i == 2 else []), mm, D[i], T.K0[:, 15 - u:143 - u],
+                 T.X1[:, J * i + u:J * i + J:16], u == 0, False)
+        call("Y%d" % i, ["BH", "IDN"], mm, D[i], T.IDN[:], T.BH[:, blk(i)], False, True)
+    call("E16", ["o0", "o1", "o2"], ts, T.E16[:], T.S[:], 0.125, None, OP.mult)
+
+    for i in range(3):
+        c = lambda s: s + str(i)
+        call(c("M"), [c("Y"), "EE"], tt, T.M1[:, blk(i)], T.EE[:, blk(i)], D[i], OP.min)
+        call(c("C"), [c("M")], ts, T.C2[:, blk(i)], T.M1[:, blk(i)], 2046 if i < 2 else 2047, None, AND)
+        call(c("S"), [c("C"), "Q6"], tt, (T.S2 if i < 2 else T.G)[:, blk(i)], T.C2[:, blk(i)], Q8, OP.add)
+        if i < 2:
+            call(c("L"), [c("S")], ts, T.S16[:, blk(i)], T.S2[:, blk(i)], 0.5, None, OP.mult)
+            call(c("P"), [c("M")], ts, T.PAR[:, blk(i)], T.M1[:, blk(i)], 1, None, AND)
+            call(c("G"), [c("S"), c("P")], tt, T.G[:, blk(i)], T.S2[:, blk(i)], T.PAR[:, blk(i)], OP.add)
+            call(c("F"), [c("P")], ts, T.PP[:, blk(i)], T.PAR[:, blk(i)], float(-15 * (4096 >> (r + 4))), float(4096 >> r), OP.mult, OP.add)
+    seen = ["sw0", "sw1", ("sn", 2 * len(on)), ("s0", len(off)), ("s1", len(off)), ("fs", hs)]
+    call("h0", ["L0"] + seen, copy, T.X2[:, pos(0)], T.SW[:].indirect(T.S16[:, blk(0)]), AF.Copy)
+    call("ha", ["L1"] + seen, copy, T.X2[:, pos(1, HV)], T.SW[:].indirect(T.S16[:, 48 + HV:96]), AF.Copy)
+    call("hv", ["L1"] + seen, cp, T.X2[:, pos(1, 0, HV)], T.SW[:].indirect(T.S16[:, 48:48 + HV]))
+    for u in range(16):
+        call("z%d" % u, ["h0", "ha", "hv", "d%d" % u], mm, T.HU[:, two], T.DG[:, 128 * u:128 * u + 128], T.X2[:, u:2 * J:16], u == 0, u == 15)
+
+    E1, E2, T1, T2 = (T.HP[:, 64 * i:64 * i + 48] for i in range(4))
+    call("e1", ["G0", "G1", "sw0"], tt, E1, T.G[:, blk(1)], T.G[:, blk(0)], OP.subtract)
+    call("e2", ["S2", "G1", "sw0"], tt, E2, T.G[:, blk(2)], T.G[:, blk(1)], OP.subtract)
+    call("TK", ["z15", "F0", "F1"], tt, T.TK[:], T.HU[:, two], T.PP[:], OP.mult)
+    call("KB", ["TK"], ts, T.KB[:], T.TK[:], 12, 1, SHR, AND)
+    call("KK", ["KB"], tt, T.KK[:], T.KB[:, blk(0)], T.KB[:, blk(1)], OP.mult)
+    call("f1", ["KB", "e1"], tt, T1, T.KB[:, blk(0)], E1, OP.mult) if False else call("f1", ["KB", "e1"], tt, T.W[:], T.KB[:, blk(0)], E1, OP.mult)
+    call("f2", ["KK", "e2"], tt, T.KK[:], T.KK[:], E2, OP.mult)
+    call("f3", ["f1", "G0"], tt, T1, T.W[:], T.G[:, blk(0)], OP.add)
+    call("X", ["f2", "f3"], tt, T.X[:], T.KK[:], T1, OP.add)
+    call("X16", ["X"], cp, T.X16[:], T.X[:])
+
+    here = ["X16", ("lvec", 16), ("vp", len(on))] + [("x%d" % c, len(off)) for c in range(n)] + [("fw", handed)]
+    call("ya", here, copy, T.Y[:, 16 * YV:768], T.VW[:].indirect(T.X16[:, YV:48]), AF.Copy)
+    call("yv", here, cp, T.Y[:, 0:16 * YV], T.VW[:].indirect(T.X16[:, 0:YV]))
+
+    for q in "vat":
+        for name in ORDER[q].split():
+            deps, fn, args, kw = todo.pop(name)
+            need(q, deps)
+            fn(*args, **kw).then_inc(T.sem[q], 1)
+
+    need("s", ["X"])
+    g.sync.dma_start(T.chosen[:], T.X[:]).then_inc(T.sem.st, 16)
+    need("a", ["ya"])
     act.dma_start(T.y[:, 16 * YV:768], T.Y[:, 16 * YV:768]).then_inc(T.sem.st, 16)
-    need("s", [yv])
+    need("s", ["yv"])
     g.sync.dma_start(T.y[:, 0:16 * YV], T.Y[:, 0:16 * YV]).then_inc(T.sem.st, 16)
 
-    need("p", [(q, cnt[q]) for q in ("v", "a", "t", "p")])
-    need("p", [("ls", (2 + n) * 16), ("lf", handed), ("vp", n * len(on)), ("fw", handed), ("pk", 16), ("sn", 16), ("st", 48)])
-    need("p", [("lsd", 16), ("ltab", 32), ("lrk", 16), ("lseen", 16), ("lvec", 16)])
+    need("p", [(q, len(ORDER[q].split())) for q in "vatp"])
+    sent = len(off) + len(on) + 2 * (len(off) + len(on)) + n * len(off) + len(on)
+    need("p", [("ls", sent), ("lf", hs + handed), ("vp", len(on)), ("fw", handed), ("fs", hs), ("pk", 16), ("sn", 2 * len(on)), ("st", 48)])
+    need("p", [("lsd", 16), ("ltab", 32), ("lrk", 16), ("ls0", 16), ("ls1", 16), ("lvec", 16)])

from concourse.bass import DstId, RemoteDMATransfer
from concourse.mybir import AluOpType as OP, ActivationFunctionType as AF

M, K, N = 2048, 48, 4
J = 16 * K
CUTS = (0, 896, 1536, 2048)
YV = 24
HV = 24
LOOKS = (((0, 48),), ((0, 48),), ((0, 24), (24, 48)))
ORDER = {
    "p": "pu n0 cp n1 ei cb p8",
    "v": "TM TA PB sf ID MOD s0 tab s1 l0 si MW l1 m0 ra sg m1 E8 KZ r1 t0 r0 r2 t1 b0 b1 c0 c1 a0 a1 TS W H VV PC HH "
         "u0 u1 u2 u3 u4 u5 u6 K0 LO o2 o1 o0 BH E16 IDN EE x00 x10 x20 M0 C0 S0 L0 P0 M1 x21 C1 F0 S1 L1 G0 hv P1 M2 C2 G1 S2 "
         "e1 e2 F1 TK KB f1 KK f3 f2 X X16 yv",
    "a": "d9 d14 d12 d1 d13 i6 cw d2 q0 q1 d11 d7 d0 d8 sw0 d15 sw1 k0 k1 k2 d3 d6 d4 d10 d5 h0 ha ya",
    "t": " ".join(["pe0 po0 pe1 po1 rt"] + ["Q%d" % w for w in range(7)]
                  + [" ".join(["y%d_%d" % (i, u) for u in range(16)] + ["Y%d" % i]) for i in range(3)] + ["z%d" % u for u in range(16)])}

I4, F4, F2, H2, U2 = "int32", "float32", "bfloat16", "float16", "uint16"
SCRATCH = {n: ("sbuf", [p, c], d) for n, p, c, d in (
    ("PW", 128, 1024, I4), ("SW", 128, 4096, F2), ("VW", 128, 8192, F2), ("SEEN", 128, 2048, F2), ("SDI", 128, 1, I4),
    ("RKI", 8, 8, I4), ("RKA", 8, 4, F4), ("RT", 8, 11, F4), ("TI", 128, 16, I4), ("TA", 128, 24, I4), ("T8", 128, 8, I4),
    ("TS", 128, 8, I4), ("MI", 128, 128, F4), ("N0", 128, 192, I4), ("EI", 8, 128, F4), ("PB", 128, 1, I4),
    ("PC", 128, 1, F4), ("K0", 128, 144, H2), ("ID", 128, 128, F2), ("ID16", 128, 128, F2), ("IDN", 128, 128, H2),
    ("E8L", 8, 128, F4), ("MOD", 128, 16, F4), ("MW", 128, 8, F2), ("DG", 128, 2048, F2), ("SI", 128, 1, I4), ("SF", 128, 2, F4),
    ("L0", 128, 192, I4), ("L", 128, 192, I4), ("LL", 128, 192, F4), ("TT", 128, 192, I4), ("B", 128, 192, I4),
    ("BB", 128, 192, I4), ("AA", 128, 192, I4), ("H", 128, 144, I4), ("H16", 128, 144, U2), ("W12", 128, 48, I4),
    ("VV", 128, 48, I4), ("TM", 128, 336, F2), ("CW", 8, 4, F4), ("CB", 8, 4, F4),
    ("LOW8", 128, 144, I4), ("EE", 128, 144, I4), ("BH", 128, 144, H2),
    ("S", 128, 144, I4), ("E16", 128, 144, U2), ("MK", 128, 2304, F2), ("X1", 128, 2304, H2), ("X2", 128, 1536, F2),
    ("M1", 128, 144, I4), ("C2", 128, 144, I4), ("S2", 128, 144, I4), ("S16", 128, 96, U2), ("PAR", 128, 96, I4), ("G", 128, 144, I4),
    ("PP", 128, 96, I4), ("TK", 128, 96, I4), ("KK", 128, 48, F4), ("KB", 128, 96, I4), ("X", 128, 48, F4), ("W", 128, 48, F4),
    ("X16", 128, 48, U2), ("Y", 128, 768, F2))}
SCRATCH["HP"] = ("psum", [128, 1024], F4)
SCRATCH["HU"] = ("psum", [128, 512], F4)
SCRATCH["DD"] = ("psum", [128, 1024], F4)
SCRATCH["RQ"] = ("psum", [128, 512], F4)
SCRATCH["VB"] = ("psum", [128, 512], F4)
SEMAPHORES = ["v", "a", "t", "p", "lsd", "ltab", "lrk", "ls0", "ls1", "lvec", "pk", "sn", "vp", "s0", "s1", "fs", "x0", "x1", "x2", "fw",
              "ls", "lf", "st"]


def rank_program(g, core, T, topo):
    r = T.rank_of(core)
    if r is None:
        return
    others = [c for c in T.cores if c != core]
    partner = [c for c in others if c in topo.cores_of(core)][0]
    cross = [c for c in others if c != partner and topo.die(c) == topo.die(core)][0]
    diag = [c for c in others if c not in (partner, cross)][0]
    off = topo.engines(core, cross)
    near = topo.engines(core, partner)
    on = [e for e in near if e not in off]
    bits = lambda es: sum(1 << e for e in es)
    half = len(off) // 2
    lanes = {partner: bits(on), cross: bits(off[:half]), diag: bits(off[half:])}
    vec, act, pe = g.vector, g.scalar, g.tensor
    eng = {"v": vec, "a": act, "t": pe, "p": g, "s": g.sync}
    place = {name: (q, i + 1) for q in ORDER for i, name in enumerate(ORDER[q].split())}
    todo = {}
    lvl = {q: {} for q in eng}

    def need(q, deps):
        for d in deps:
            s, n = place[d] if d in place else d
            if lvl[q].get(s, 0) < n:
                eng[q].wait_ge(T.sem[s], n)
                lvl[q][s] = n

    def call(name, deps, f, *args, **kw):
        todo[name] = (deps, f, args, kw)

    def blk(i):
        return slice(48 * i, 48 * i + 48)

    def pos(i, a=0, b=48):
        return slice(J * i + 16 * a, J * i + 16 * b)

    ts, tt, cp, copy, mm = vec.tensor_scalar, vec.tensor_tensor, vec.tensor_copy, act.activation, pe.matmul
    SHR, AND = OP.arith_shift_right, OP.bitwise_and
    two, last = slice(0, 96), slice(48, 192)
    halves = (slice(0, 96), slice(96, 192))

    my = slice(256 * r, 256 * r + 256)
    g.sync.dma_start(T.SDI[:], T.sd[:]).then_inc(T.sem.lsd, 16)
    act.dma_start(T.PW[1:128:2, my], T.ali[:]).then_inc(T.sem.ltab, 16)
    g.sync.dma_start(T.PW[0:128:2, my], T.thr[:]).then_inc(T.sem.ltab, 16)
    act.dma_start(T.RKI[:], T.rk[:]).then_inc(T.sem.lrk, 16)
    for h in range(2):
        w = slice(1024 * h, 1024 * h + 1024)
        g.sync.dma_start(T.SEEN[:, w], T.seen[:, w]).then_inc(T.sem["ls%d" % h], 16)
    g.sync.dma_start(T.VW[:, M * r:M * r + M], T.vec[:]).then_inc(T.sem.lvec, 16)

    f = {"allow_small_or_imprecise_dtypes": True}

    def ramp(*args, **kw):
        g.iota(*args, **kw).then_inc(T.sem.p, 1)

    def send(buf, a0, a1, dests):
        tr = []
        for d, mask, s in dests:
            rid, pid = topo.addr(d, core)
            tr.append(RemoteDMATransfer(dst_ids=[DstId(rid=rid, pnc=pid)], dma_engine_mask=mask, remote_sem=T.sem[s],
                                        srcs=[T[buf][:, a0:a1]], dsts=[T[buf][:, a0:a1]]))
        g.remote_dma_fused(tr, local_sem=T.sem.ls)

    def hand(buf, a0, a1, s, es):
        rid, pid = topo.addr(partner, core)
        g.remote_dma(T[buf][:, a0:a1], T[buf][:, a0:a1], T.sem[s], T.sem.lf, pid, rid, bits(es))

    ramp(T.TI[:, 0:16], [[-1, 16]], 0, 1)
    ramp(T.N0[:, 0:96], [[1597, 2], [6388, 48]], -(1 << 23), 0)
    ramp(T.MI[:], [[1, 128]], 0, -1, **f)
    ramp(T.N0[:, 96:192], [[1597, 2], [6388, 48]], 2 * 1597 - (1 << 23), 0)
    ramp(T.EI[:], [[16, 8], [0, 16]], 0, -16, **f)
    ramp(T.CB[:], [[4096, 4]], 0, 0, **f)
    far = T.rank_of(cross)
    need("p", ["tab"])
    send("PW", 256 * r, 256 * r + 256, [(d, lanes[d], "pk") for d in (cross, diag, partner)])
    ramp(T.T8[:], [[-16, 8]], 0, 1)
    for h in range(2):
        need("p", ["sw%d" % h])
        o = 1024 * r + 512 * h
        send("SW", o, o + 512, [(cross, bits(off), "s%d" % h), (partner, bits(on), "sn")])
    need("p", [("lvec", 16)])
    pieces = list(zip(CUTS, CUTS[1:]))
    n = len(pieces)
    for c, (a0, a1) in enumerate(pieces):
        send("VW", M * r + a0, M * r + a1, [(cross, bits(off), "x%d" % c)])
    for h in range(2):
        need("p", [("s%d" % h, len(off))])
        o = 1024 * far + 512 * h
        hand("SW", o, o + 512, "fs", on)
    send("VW", M * r, M * r + M, [(partner, bits(on), "vp")])
    for c, (a0, a1) in enumerate(pieces):
        need("p", [("x%d" % c, len(off))])
        hand("VW", M * far + a0, M * far + a1, "fw", near)
    hs, handed = 2 * len(on), n * len(near)

    call("TA", ["pu"], ts, T.TA[:, 0:16], T.TI[:, 0:16], 15, None, AND)
    call("MOD", ["TA"], ts, T.MOD[:], T.TA[:, 0:16], 0.0, None, OP.is_equal)
    call("PB", ["pu"], ts, T.PB[:], T.TI[:, 0:1], 1, None, AND)
    call("PC", ["PB"], ts, T.PC[:], T.PB[:], -4095.0, 4096.0, OP.mult, OP.add)
    call("TM", ["pu"], ts, T.TA[:, 16:24], T.TI[:, 0:16:2], 15, None, AND)
    call("MW", ["TM"], ts, T.MW[:], T.TA[:, 16:24], 1.0, None, OP.is_le)
    call("ID", ["cp"], ts, T.ID[:], T.MI[:], 0.0, None, OP.is_equal)
    call("IDN", ["ID"], ts, T.IDN[:], T.ID[:], -4096.0, None, OP.mult)
    call("KZ", ["n0", "n1"], ts, T.K0[:], T.N0[:, 0:144], 0.0, None, OP.mult)
    call("TS", ["p8"], ts, T.TS[:], T.T8[:], 4, None, SHR)
    call("K0", ["KZ", "TS", "PC"], ts, T.K0[:, 15:143:16], T.TS[:], 0.0, T.PC[:], OP.is_equal, OP.mult)
    call("E8", ["ei"], ts, T.E8L[:], T.EI[:], 0.0, None, OP.is_equal)
    call("i6", ["ID"], copy, T.ID16[:], T.ID[:], AF.Copy, scale=16.0)
    for u in range(16):
        call("d%d" % u, ["ID", "MOD"], copy, T.DG[:, 128 * u:128 * u + 128], T.ID[:], AF.Copy, scale=T.MOD[:, u:u + 1])

    call("tab", [("ltab", 32)], ts, T.PW[:, my], T.PW[:, my], -2048.0, None, OP.add)
    for h in range(2):
        o, c = T.HP[:, 512 * h:512 * h + 512], 1024 * h
        call("pe%d" % h, ["ID", ("ls%d" % h, 16)], mm, o, T.ID[:], T.SEEN[:, c:c + 1024:2], True, False)
        call("po%d" % h, ["i6", ("ls%d" % h, 16)], mm, o, T.ID16[:], T.SEEN[:, c + 1:c + 1024:2], False, True)
        call("sw%d" % h, ["po%d" % h], copy, T.SW[:, 1024 * r + 512 * h:1024 * r + 512 * h + 512], o, AF.Copy)
    call("cw", ["cb"], copy, T.CW[:], T.CB[:], AF.Copy, scale=0.5)
    call("ra", [("lrk", 16)], ts, T.RKA[:], T.RKI[:, 4:8], 2048.0, None, OP.mult)
    call("r0", [("lrk", 16), "cb"], tt, T.RT[:, 0:4], T.RKI[:, 0:4], T.CB[:], OP.add)
    call("r1", ["ra", "cw"], tt, T.RT[:, 4:8], T.RKA[:], T.CW[:], OP.subtract)
    call("r2", ["ra", "cw"], tt, T.RT[:, 8:11], T.CW[:, 1:4], T.RKA[:, 0:3], OP.subtract)
    call("rt", ["E8", "r0", "r1", "r2"], mm, T.DD[:, 960:971], T.E8L[:], T.RT[:], True, True)

    call("sf", [("lsd", 16)], cp, T.SF[:, 0:1], T.SDI[:])
    call("si", [("lsd", 16)], ts, T.SI[:], T.SDI[:], 12, None, SHR)
    call("sg", ["si"], ts, T.SF[:, 1:2], T.SI[:], 64.0, -262144.0, OP.mult, OP.add)
    for h, w in enumerate(halves):
        l64 = (T.VB[:, 0:96], T.HU[:, 256:352])[h]
        i = lambda s: s + str(h)
        call(i("s"), ["sf", i("n")], ts, T.L0[:, w], T.N0[:, w], T.SF[:, 0:1], None, OP.add)
        call(i("l"), [i("s")], ts, T.L[:, w], T.L0[:, w], 4095, None, AND)
        call(i("m"), [i("l")], ts, l64, T.L[:, w], 64.0, -262144.0, OP.mult, OP.add)
        call(i("q"), [i("m")], copy, T.LL[:, w], l64, AF.Square, bias=4096.0, scale=1.0 / 64)
        call(i("t"), [i("q"), "sg"], ts, T.TT[:, w], T.LL[:, w], T.SF[:, 1:2], None, OP.add)
        call(i("b"), [i("t")], ts, T.B[:, w], T.TT[:, w], 6, 4095, SHR, AND)
        call(i("c"), [i("b")], tt, T.BB[:, w], T.B[:, w], T.B[:, w], OP.mult)
        call(i("a"), [i("c")], tt, T.AA[:, w], T.BB[:, w], l64, OP.add)
    call("H", ["a0", "a1"], ts, T.H[:], T.AA[:, last], 15, 7, SHR, AND)
    call("HH", ["H"], cp, T.H16[:], T.H[:])
    call("LO", ["a0", "a1"], ts, T.LOW8[:], T.AA[:, last], 4, 255 << 3, SHR, AND)
    call("EE", ["a0", "a1"], ts, T.EE[:], T.AA[:, last], 7, 2047, SHR, AND)
    call("BH", ["b0", "b1"], ts, T.BH[:], T.B[:, last], -2048.0, None, OP.add)

    Q8 = T.RQ[:, 0:48]
    call("W", ["a0"], ts, T.W12[:], T.AA[:, 0:48], 4, 3 << 12, SHR, AND)
    call("VV", ["W", "b0"], tt, T.VV[:], T.W12[:], T.B[:, 0:48], OP.add)
    for w in range(7):
        lim = T.DD[:, 960 + w:961 + w] if w < 4 else 4096.0 * (w - 3)
        call("u%d" % w, ["VV", "rt"], ts, T.TM[:, blk(w)], T.VV[:], lim, T.DD[:, 964 + w:965 + w], OP.is_ge, OP.mult)
        call("Q%d" % w, ["ID", "u%d" % w], mm, Q8, T.ID[:], T.TM[:, blk(w)], w == 0, w == 6)

    D = [T.DD[:, 0:48], T.DD[:, 512:560], T.DD[:, 48:96]]
    for i in range(3):
        call("o%d" % i, ["Q6", "LO"], tt, T.S[:, blk(i)], T.LOW8[:, blk(i)], Q8, OP.add)
        call("k%d" % i, ["HH", "MW"], copy, T.MK[:, pos(i)], T.MW[:].indirect(T.H16[:, blk(i)]), AF.Copy)
        for c, (a, b) in enumerate(LOOKS[i]):
            call("x%d%d" % (i, c), [("pk", 16), "tab", "k%d" % i, "E16"], tt, T.X1[:, pos(i, a, b)],
                 T.PW[:].indirect(T.E16[:, 48 * i + a:48 * i + b]), T.MK[:, pos(i, a, b)], OP.mult)
        done = ["x%d%d" % (i, c) for c in range(len(LOOKS[i]))]
        for u in range(16):
            call("y%d_%d" % (i, u), done + ["K0"] + (["M0"] if i == 2 else []), mm, D[i], T.K0[:, 15 - u:143 - u],
                 T.X1[:, J * i + u:J * i + J:16], u == 0, False)
        call("Y%d" % i, ["BH", "IDN"], mm, D[i], T.IDN[:], T.BH[:, blk(i)], False, True)
    call("E16", ["o0", "o1", "o2"], ts, T.E16[:], T.S[:], 0.125, None, OP.mult)

    for i in range(3):
        c = lambda s: s + str(i)
        call(c("M"), [c("Y"), "EE"], tt, T.M1[:, blk(i)], T.EE[:, blk(i)], D[i], OP.min)
        call(c("C"), [c("M")], ts, T.C2[:, blk(i)], T.M1[:, blk(i)], 2046 if i < 2 else 2047, None, AND)
        call(c("S"), [c("C"), "Q6"], tt, (T.S2 if i < 2 else T.G)[:, blk(i)], T.C2[:, blk(i)], Q8, OP.add)
        if i < 2:
            call(c("L"), [c("S")], ts, T.S16[:, blk(i)], T.S2[:, blk(i)], 0.5, None, OP.mult)
            call(c("P"), [c("M")], ts, T.PAR[:, blk(i)], T.M1[:, blk(i)], 1, None, AND)
            call(c("G"), [c("S"), c("P")], tt, T.G[:, blk(i)], T.S2[:, blk(i)], T.PAR[:, blk(i)], OP.add)
            call(c("F"), [c("P")], ts, T.PP[:, blk(i)], T.PAR[:, blk(i)], float(-15 * (4096 >> (r + 4))), float(4096 >> r), OP.mult, OP.add)
    seen = ["sw0", "sw1", ("sn", 2 * len(on)), ("s0", len(off)), ("s1", len(off)), ("fs", hs)]
    call("h0", ["L0"] + seen, copy, T.X2[:, pos(0)], T.SW[:].indirect(T.S16[:, blk(0)]), AF.Copy)
    call("ha", ["L1"] + seen, copy, T.X2[:, pos(1, HV)], T.SW[:].indirect(T.S16[:, 48 + HV:96]), AF.Copy)
    call("hv", ["L1"] + seen, cp, T.X2[:, pos(1, 0, HV)], T.SW[:].indirect(T.S16[:, 48:48 + HV]))
    for u in range(16):
        call("z%d" % u, ["h0", "ha", "hv", "d%d" % u], mm, T.HU[:, two], T.DG[:, 128 * u:128 * u + 128], T.X2[:, u:2 * J:16], u == 0, u == 15)

    E1, E2, T1, T2 = (T.HP[:, 64 * i:64 * i + 48] for i in range(4))
    call("e1", ["G0", "G1", "sw0"], tt, E1, T.G[:, blk(1)], T.G[:, blk(0)], OP.subtract)
    call("e2", ["S2", "G1", "sw0"], tt, E2, T.G[:, blk(2)], T.G[:, blk(1)], OP.subtract)
    call("TK", ["z15", "F0", "F1"], tt, T.TK[:], T.HU[:, two], T.PP[:], OP.mult)
    call("KB", ["TK"], ts, T.KB[:], T.TK[:], 12, 1, SHR, AND)
    call("KK", ["KB"], tt, T.KK[:], T.KB[:, blk(0)], T.KB[:, blk(1)], OP.mult)
    call("f1", ["KB", "e1"], tt, T1, T.KB[:, blk(0)], E1, OP.mult) if False else call("f1", ["KB", "e1"], tt, T.W[:], T.KB[:, blk(0)], E1, OP.mult)
    call("f2", ["KK", "e2"], tt, T.KK[:], T.KK[:], E2, OP.mult)
    call("f3", ["f1", "G0"], tt, T1, T.W[:], T.G[:, blk(0)], OP.add)
    call("X", ["f2", "f3"], tt, T.X[:], T.KK[:], T1, OP.add)
    call("X16", ["X"], cp, T.X16[:], T.X[:])

    here = ["X16", ("lvec", 16), ("vp", len(on))] + [("x%d" % c, len(off)) for c in range(n)] + [("fw", handed)]
    call("ya", here, copy, T.Y[:, 16 * YV:768], T.VW[:].indirect(T.X16[:, YV:48]), AF.Copy)
    call("yv", here, cp, T.Y[:, 0:16 * YV], T.VW[:].indirect(T.X16[:, 0:YV]))

    for q in "vat":
        for name in ORDER[q].split():
            deps, fn, args, kw = todo.pop(name)
            need(q, deps)
            fn(*args, **kw).then_inc(T.sem[q], 1)

    need("s", ["X"])
    g.sync.dma_start(T.chosen[:], T.X[:]).then_inc(T.sem.st, 16)
    need("a", ["ya"])
    act.dma_start(T.y[:, 16 * YV:768], T.Y[:, 16 * YV:768]).then_inc(T.sem.st, 16)
    need("s", ["yv"])
    g.sync.dma_start(T.y[:, 0:16 * YV], T.Y[:, 0:16 * YV]).then_inc(T.sem.st, 16)

    need("p", [(q, len(ORDER[q].split())) for q in "vatp"])
    sent = len(off) + len(on) + 2 * (len(off) + len(on)) + n * len(off) + len(on)
    need("p", [("ls", sent), ("lf", hs + handed), ("vp", len(on)), ("fw", handed), ("fs", hs), ("pk", 16), ("sn", 2 * len(on)), ("st", 48)])
    need("p", [("lsd", 16), ("ltab", 32), ("lrk", 16), ("ls0", 16), ("ls1", 16), ("lvec", 16)])
